import numpy as np
import ml_dtypes


def mxq(x, axis, fmt="e4m3"):
    dtype, down = {"e4m3": (ml_dtypes.float8_e4m3fn, 7), "e5m2": (ml_dtypes.float8_e5m2, 14)}[fmt]
    v = np.moveaxis(np.asarray(x, np.float32).astype(ml_dtypes.bfloat16).astype(np.float64), axis, -1)
    blocks = v.reshape(v.shape[:-1] + (-1, 32))
    amax = np.abs(blocks).max(-1, keepdims=True)
    byte = np.maximum(np.where(amax > 0, np.frexp(amax)[1] - 1 + 127, 0) - down, 1)
    scale = np.exp2(byte - 127.0)
    codes = (blocks / scale).astype(np.float32).astype(dtype).astype(np.float64)
    return np.moveaxis((codes * scale).reshape(v.shape), -1, axis)


WIDE = False


def mx_kscale(k):
    if not WIDE:
        return np.ones(k)
    levels = np.array([10, -10, 5, -5, 0])
    if k % 512:
        return np.exp2(np.random.permutation(np.resize(levels, k // 32))).repeat(32)
    a = np.empty((k // 512, 16))
    for p in range(k // 512):
        a[p, :8] = np.random.permutation(np.resize(levels, 8))
        for g in range(8):
            far = levels[np.abs(levels - a[p, g]) >= 10]
            a[p, g + 8] = far[np.random.randint(len(far))]
    return np.exp2(a.ravel()).repeat(32)


def f64(x):
    return np.asarray(x).astype(np.float64)


def striped(idx):
    return np.tile(np.asarray(idx).reshape(-1, 16).T, (8, 1)).astype(np.uint16)


def unstriped(offs):
    return offs[:16].T.reshape(-1).astype(np.int64)


E2M1 = np.array([0.0, 0.5, 1.0, 1.5, 2.0, 3.0, 4.0, 6.0, -0.0, -0.5, -1.0, -1.5, -2.0, -3.0, -4.0, -6.0])


def pack_weight(w, fmt):
    k, n = w.shape
    w = f64(np.asarray(w, np.float32).astype(ml_dtypes.bfloat16)).reshape(k // 32, 32, n)
    amax = np.abs(w).max(1)
    if fmt == "e4m3":
        byte = np.frexp(amax)[1] - 1 + 127 - 7
    else:
        mant, ex = np.frexp(amax / 6.0)
        byte = np.where(mant > 0.5, ex, ex - 1) + 127
    byte = np.clip(np.where(amax > 0, byte, 1), 1, 254)
    scaled = (w * np.exp2(127.0 - byte)[:, None, :]).reshape(k, n).astype(np.float32)
    by_word = np.ascontiguousarray(scaled.reshape(k // 512, 128, 4, n).transpose(0, 1, 3, 2))
    if fmt == "e4m3":
        words = by_word.astype(ml_dtypes.float8_e4m3fn).view(np.uint8)
    else:
        c = by_word.astype(ml_dtypes.float4_e2m1fn).view(np.uint8) & 0xF
        words = (c[..., 0::2] | (c[..., 1::2] << 4)).reshape(k // 512, 128, 2 * n)
    return np.ascontiguousarray(words), np.ascontiguousarray(byte.astype(np.uint8).reshape(k // 512, 16, n))


def unpack_weight(words, scales, fmt):
    g, _, n = scales.shape
    words = np.ascontiguousarray(words).reshape(g, 128, n, -1)
    if fmt == "e4m3":
        vals = words.view(ml_dtypes.float8_e4m3fn).astype(np.float64)
    else:
        nib = np.empty((g, 128, n, 4), np.uint8)
        nib[..., 0::2] = words & 0xF
        nib[..., 1::2] = words >> 4
        vals = E2M1[nib]
    vals = vals * np.repeat(np.exp2(scales.astype(np.float64) - 127.0), 8, axis=1)[..., None]
    return vals.transpose(0, 1, 3, 2).reshape(g * 512, n)


B, N, T, D, NQ = 2, 512, 2048, 1024, 128


def setup_inputs():
    n = np.random.standard_normal
    jdx = np.random.permutation(1024)[:B * NQ]
    pages = np.random.permutation(T // 64)[:B * N // 64]
    idx = (pages[:, None] * 64 + np.arange(64)[None, :]).reshape(-1)
    s = mx_kscale(D)[:, None]
    kp = pack_weight(n((D, T)) / s, "e2m1")
    return {
        "qT": (n((D, 1024)) * s * (1.00 / np.sqrt(D))).astype(np.float32),
        "k_words": np.ascontiguousarray(kp[0].reshape(1, 2, 128, T, 2).transpose(0, 2, 3, 1, 4)).reshape(1, 128, T, 4),
        "k_scales": kp[1],
        "kb": np.tile(n(2048), (128, 1)).astype(np.float32),
        "offq": striped(jdx),
        "offs": striped(idx),
    }


def reference(qT, k_words, k_scales, kb, offq, offs):
    jdx = unstriped(offq)
    idx = unstriped(offs)
    pick = lambda x, which: x[:, which].reshape(x.shape[0], B, -1).transpose(1, 0, 2)
    qg = mxq(pick(f64(qT), jdx), 1, "e4m3")
    k = unpack_weight(k_words.reshape(1, 128, T, 2, 2).transpose(0, 3, 1, 2, 4).reshape(2, 128, 2 * T), k_scales, "e2m1")
    kg = pick(k, idx)
    qq = qg
    a = qq.transpose(0, 2, 1) @ kg
    y = a + pick(f64(kb), idx)[:, :1, :]
    return y

@@ -1,0 +1,144 @@
+from contextlib import ExitStack
+
+import concourse.mybir as mybir
+from concourse.masks import make_identity
+
+F32 = mybir.dt.float32
+BF16 = mybir.dt.bfloat16
+I32 = mybir.dt.int32
+U32 = mybir.dt.uint32
+U16 = mybir.dt.uint16
+U8 = mybir.dt.uint8
+FP8X4 = mybir.dt.float8_e4m3fn_x4
+FP4X4 = mybir.dt.float4_e2m1fn_x4
+ADD = mybir.AluOpType.add
+
+B, N, T, D, NQ, POOL = 2, 512, 2048, 1024, 128, 1024
+P = 128
+PACK = 4
+PASSES = D // (P * PACK)
+SLOTS = B * N
+QUERIES = B * NQ
+BIAS_ROW = 16
+HALF = N // 2
+
+FLOPS = 2 * B * NQ * N * D
+
+
+def tile_attend_lq_score_kernel(tc, qT, k_words, k_scales, kb, offq, offs, out):
+    nc = tc.nc
+    with ExitStack() as ctx:
+        keep = ctx.enter_context(tc.tile_pool(name="keep", bufs=1))
+        psum = ctx.enter_context(tc.psum_pool(name="psum", bufs=1))
+
+        slot_list = keep.tile([P, SLOTS // 16], U16, name="slot_list")
+        query_list = keep.tile([P, QUERIES // 16], U16, name="query_list")
+        scale_pool = keep.tile([P, PASSES * T // 4], I32, name="scale_pool", align_bytes=64)
+        bias_pool = keep.tile([P, T], F32, name="bias_pool", align_bytes=64)
+        word_pool = keep.tile([P, T], I32, name="word_pool", align_bytes=64)
+        planes = [keep.tile([P, POOL], F32, name="plane%d" % i, align_bytes=64) for i in range(PASSES * PACK)]
+        q_rows = qT.rearrange("(o p t) c -> o t p c", o=PASSES, t=PACK)
+
+        def load_plane(i):
+            nc.sync.dma_start(planes[i][:], q_rows[i // PACK, i % PACK])
+
+        nc.vector.memset(scale_pool[:], 0)
+        nc.vector.memset(bias_pool[:], 0.0)
+        nc.sync.dma_start(slot_list[:], offs)
+        nc.sync.dma_start(query_list[:], offq)
+        load_plane(0)
+        scale_rows = k_scales.bitcast(I32).rearrange("o (q r) w -> r q o w", r=4)
+        for r in range(4):
+            nc.sync.dma_start(scale_pool[r:P:32, :].rearrange("q (o w) -> q o w", o=PASSES), scale_rows[r])
+        nc.sync.dma_start(word_pool[:], k_words[0].rearrange("p t b -> p (t b)").bitcast(I32))
+        nc.sync.dma_start(bias_pool[BIAS_ROW : BIAS_ROW + 1, :], kb[0:1, :])
+        for i in range(1, PASSES * PACK):
+            load_plane(i)
+
+        identity = keep.tile([P, P], F32, name="identity", align_bytes=64)
+        make_identity(nc, identity[:])
+
+        picked = [keep.tile([P, PACK, QUERIES], F32, name="picked%d" % o, align_bytes=64) for o in range(PASSES)]
+        grouped = [keep.tile([P, QUERIES, PACK], BF16, name="grouped%d" % o, align_bytes=64) for o in range(PASSES)]
+        q_codes = [keep.tile([P, QUERIES], U32, name="q_codes%d" % o, align_bytes=64) for o in range(PASSES)]
+        q_scales = [keep.tile([P, QUERIES], U8, name="q_scales%d" % o, align_bytes=64) for o in range(PASSES)]
+        key_pairs = keep.tile([P, SLOTS], U32, name="key_pairs", align_bytes=64)
+        key_words = [keep.tile([P, 2 * SLOTS], U8, name="key_words%d" % o, align_bytes=64) for o in range(PASSES)]
+        key_scales = [keep.tile([P, SLOTS], U8, name="key_scales%d" % o, align_bytes=64) for o in range(PASSES)]
+        bias_row = keep.tile([P, SLOTS], F32, name="bias_row", align_bytes=64)
+        bias_cols = keep.tile([P, SLOTS // P], F32, name="bias_cols", align_bytes=64)
+        bias = [keep.tile([P, N], F32, name="bias%d" % b, align_bytes=64) for b in range(B)]
+        result = [keep.tile([P, N], F32, name="result%d" % b, align_bytes=64) for b in range(B)]
+        turned = [psum.tile([P, N // P, P], F32, name="turned%d" % b) for b in range(B)]
+        spread = [psum.tile([P, N], F32, name="spread%d" % b) for b in range(B)]
+        scores = [psum.tile([P, N], F32, name="scores%d" % b) for b in range(B)]
+
+        def pick_plane(o, t):
+            nc.vector.tensor_copy(picked[o][:, t, :], planes[PACK * o + t][:].indirect(query_list[:]))
+
+        def quantize(o, cols):
+            nc.vector.quantize_mx(
+                out=q_codes[o][:, cols].bitcast(FP8X4),
+                scales=q_scales[o][:, cols],
+                in_=grouped[o][:, cols, :].rearrange("p q t -> p (q t)"),
+            )
+
+        def multiply(o, b):
+            q_cols = slice(b * NQ, (b + 1) * NQ)
+            nc.tensor.matmul_mx(
+                out=scores[b][:],
+                lhsT=q_codes[o][:, q_cols].bitcast(FP8X4),
+                lhsT_scale=q_scales[o][:, q_cols],
+                rhs=key_words[o][:, 2 * b * N : 2 * (b + 1) * N].bitcast(FP4X4),
+                rhs_scale=key_scales[o][:, b * N : (b + 1) * N],
+                start=(o == 0),
+                stop=(o == PASSES - 1),
+            )
+
+        pick_plane(0, 0)
+        scale_bytes = scale_pool[:].bitcast(U8)
+        for o in range(PASSES):
+            nc.vector.tensor_copy(key_scales[o][:], scale_bytes[:, o * T : (o + 1) * T].indirect(slot_list[:]))
+        nc.vector.tensor_copy(key_pairs[:], word_pool[:].bitcast(U32).indirect(slot_list[:]))
+        nc.vector.tensor_copy(bias_row[:], bias_pool[:].indirect(slot_list[:]))
+
+        for b in range(B):
+            for j in range(N // P):
+                first = b * N + j * P
+                nc.tensor.transpose(turned[b][:, j, :], bias_row[:, first : first + P], identity[:])
+            nc.scalar.copy(bias_cols[:, b * (N // P) : (b + 1) * (N // P)], turned[b][:, :, BIAS_ROW])
+        for b in range(B):
+            for j in range(N // P):
+                col = b * (N // P) + j
+                nc.tensor.transpose(
+                    spread[b][:, j * P : (j + 1) * P], bias_cols[:, col : col + 1].to_broadcast([P, P]), identity[:]
+                )
+            nc.scalar.copy(bias[b][:], spread[b][:])
+
+        pick_plane(0, 1)
+        halves = key_pairs[:].bitcast(U16).rearrange("p (i o) -> p o i", o=PASSES)
+        for o in range(PASSES):
+            nc.vector.tensor_copy(key_words[o][:].bitcast(U16), halves[:, o, :])
+        pick_plane(0, 2)
+        pick_plane(0, 3)
+        nc.scalar.copy(grouped[0][:], picked[0][:].rearrange("p t q -> p q t"))
+        pick_plane(1, 0)
+        pick_plane(1, 1)
+        nc.scalar.copy(grouped[1][:, :, 0:2], picked[1][:, 0:2, :].rearrange("p t q -> p q t"))
+        quantize(0, slice(0, QUERIES))
+        for b in range(B):
+            multiply(0, b)
+        nc.vector.tensor_copy(grouped[1][:, :, 2], planes[PACK + 2][:].indirect(query_list[:]))
+        for b in range(B):
+            q_cols = slice(b * NQ, (b + 1) * NQ)
+            entries = query_list[:, b * NQ // 16 : (b + 1) * NQ // 16]
+            nc.vector.tensor_copy(grouped[1][:, q_cols, 3], planes[PACK + 3][:].indirect(entries))
+        for b in range(B):
+            quantize(1, slice(b * NQ, (b + 1) * NQ))
+            multiply(1, b)
+        for b in range(B):
+            for h in range(2):
+                cols = slice(h * HALF, (h + 1) * HALF)
+                nc.vector.tensor_tensor(result[b][:, cols], scores[b][:, cols], bias[b][:, cols], ADD)
+                queue = nc.sync if h == 0 else nc.scalar
+                queue.dma_start(out[b, :, cols], result[b][:, cols])

@@ -12,6 +12,7 @@ U8 = mybir.dt.uint8
 FP8X4 = mybir.dt.float8_e4m3fn_x4
 FP4X4 = mybir.dt.float4_e2m1fn_x4
 ADD = mybir.AluOpType.add
+COPY = mybir.ActivationFunctionType.Copy
 
 B, N, T, D, NQ, POOL = 2, 512, 2048, 1024, 128, 1024
 P = 128
@@ -19,7 +20,8 @@ PACK = 4
 PASSES = D // (P * PACK)
 SLOTS = B * N
 QUERIES = B * NQ
-BIAS_ROW = 16
+BIAS_ROW = 8
+SHIFT = 16
 HALF = N // 2
 
 FLOPS = 2 * B * NQ * N * D
@@ -33,37 +35,37 @@ def tile_attend_lq_score_kernel(tc, qT, k_words, k_scales, kb, offq, offs, out):
 
         slot_list = keep.tile([P, SLOTS // 16], U16, name="slot_list")
         query_list = keep.tile([P, QUERIES // 16], U16, name="query_list")
-        scale_pool = keep.tile([P, PASSES * T // 4], I32, name="scale_pool", align_bytes=64)
+        scale_pool = keep.tile([P, T // 4], I32, name="scale_pool", align_bytes=64)
         bias_pool = keep.tile([P, T], F32, name="bias_pool", align_bytes=64)
         word_pool = keep.tile([P, T], I32, name="word_pool", align_bytes=64)
-        planes = [keep.tile([P, POOL], F32, name="plane%d" % i, align_bytes=64) for i in range(PASSES * PACK)]
-        q_rows = qT.rearrange("(o p t) c -> o t p c", o=PASSES, t=PACK)
+        identity = keep.tile([P, P], F32, name="identity", align_bytes=64)
+        plane_pairs = [keep.tile([P, 2, POOL], F32, name="plane_pair%d" % u, align_bytes=64) for u in range(2)]
+        planes = [keep.tile([P, POOL], F32, name="plane%d" % t, align_bytes=64) for t in range(PACK)]
+        q_rows = qT.rearrange("(o p t) c -> o p t c", o=PASSES, t=PACK)
 
-        def load_plane(i):
-            nc.sync.dma_start(planes[i][:], q_rows[i // PACK, i % PACK])
-
-        nc.vector.memset(scale_pool[:], 0)
         nc.vector.memset(bias_pool[:], 0.0)
+        nc.vector.memset(scale_pool[:], 0)
+        nc.vector.memset(identity[:], 0.0)
+        make_identity(nc, identity[:], nomemset=True)
         nc.sync.dma_start(slot_list[:], offs)
         nc.sync.dma_start(query_list[:], offq)
-        load_plane(0)
+        nc.sync.dma_start(plane_pairs[0][:], q_rows[0, :, 0:2, :])
+        nc.sync.dma_start(bias_pool[BIAS_ROW : BIAS_ROW + 1, :], kb[0:1, :])
         scale_rows = k_scales.bitcast(I32).rearrange("o (q r) w -> r q o w", r=4)
         for r in range(4):
-            nc.sync.dma_start(scale_pool[r:P:32, :].rearrange("q (o w) -> q o w", o=PASSES), scale_rows[r])
+            nc.sync.dma_start(scale_pool[r:P:SHIFT, :], scale_rows[r])
         nc.sync.dma_start(word_pool[:], k_words[0].rearrange("p t b -> p (t b)").bitcast(I32))
-        nc.sync.dma_start(bias_pool[BIAS_ROW : BIAS_ROW + 1, :], kb[0:1, :])
-        for i in range(1, PASSES * PACK):
-            load_plane(i)
+        nc.sync.dma_start(plane_pairs[1][:], q_rows[0, :, 2:4, :])
+        for t in range(PACK):
+            nc.sync.dma_start(planes[t][:], q_rows[1, :, t, :])
 
-        identity = keep.tile([P, P], F32, name="identity", align_bytes=64)
-        make_identity(nc, identity[:])
-
-        picked = [keep.tile([P, PACK, QUERIES], F32, name="picked%d" % o, align_bytes=64) for o in range(PASSES)]
+        pair_pool = [keep.tile([P, POOL, 2], BF16, name="pair_pool%d" % u, align_bytes=64) for u in range(2)]
+        picked = keep.tile([P, 2, QUERIES], F32, name="picked", align_bytes=64)
         grouped = [keep.tile([P, QUERIES, PACK], BF16, name="grouped%d" % o, align_bytes=64) for o in range(PASSES)]
         q_codes = [keep.tile([P, QUERIES], U32, name="q_codes%d" % o, align_bytes=64) for o in range(PASSES)]
         q_scales = [keep.tile([P, QUERIES], U8, name="q_scales%d" % o, align_bytes=64) for o in range(PASSES)]
         key_pairs = keep.tile([P, SLOTS], U32, name="key_pairs", align_bytes=64)
-        key_words = [keep.tile([P, 2 * SLOTS], U8, name="key_words%d" % o, align_bytes=64) for o in range(PASSES)]
+        key_words = keep.tile([P, PASSES, 2 * SLOTS], U8, name="key_words", align_bytes=64)
         key_scales = [keep.tile([P, SLOTS], U8, name="key_scales%d" % o, align_bytes=64) for o in range(PASSES)]
         bias_row = keep.tile([P, SLOTS], F32, name="bias_row", align_bytes=64)
         bias_cols = keep.tile([P, SLOTS // P], F32, name="bias_cols", align_bytes=64)
@@ -73,8 +75,13 @@ def tile_attend_lq_score_kernel(tc, qT, k_words, k_scales, kb, offq, offs, out):
         spread = [psum.tile([P, N], F32, name="spread%d" % b) for b in range(B)]
         scores = [psum.tile([P, N], F32, name="scores%d" % b) for b in range(B)]
 
-        def pick_plane(o, t):
-            nc.vector.tensor_copy(picked[o][:, t, :], planes[PACK * o + t][:].indirect(query_list[:]))
+        def cast_pair(u):
+            nc.scalar.activation(pair_pool[u][:], plane_pairs[u][:].rearrange("p e c -> p c e"), COPY)
+
+        def pick_pair(u):
+            window = pair_pool[u][:].rearrange("p c e -> p (c e)").bitcast(U32)
+            words = grouped[0][:].rearrange("p q t -> p (q t)").bitcast(U32).rearrange("p (q u) -> p u q", u=2)
+            nc.vector.tensor_copy(words[:, u, :], window.indirect(query_list[:]))
 
         def quantize(o, cols):
             nc.vector.quantize_mx(
@@ -89,18 +96,16 @@ def tile_attend_lq_score_kernel(tc, qT, k_words, k_scales, kb, offq, offs, out):
                 out=scores[b][:],
                 lhsT=q_codes[o][:, q_cols].bitcast(FP8X4),
                 lhsT_scale=q_scales[o][:, q_cols],
-                rhs=key_words[o][:, 2 * b * N : 2 * (b + 1) * N].bitcast(FP4X4),
+                rhs=key_words[:, o, 2 * b * N : 2 * (b + 1) * N].bitcast(FP4X4),
                 rhs_scale=key_scales[o][:, b * N : (b + 1) * N],
                 start=(o == 0),
                 stop=(o == PASSES - 1),
             )
 
-        pick_plane(0, 0)
-        scale_bytes = scale_pool[:].bitcast(U8)
-        for o in range(PASSES):
-            nc.vector.tensor_copy(key_scales[o][:], scale_bytes[:, o * T : (o + 1) * T].indirect(slot_list[:]))
-        nc.vector.tensor_copy(key_pairs[:], word_pool[:].bitcast(U32).indirect(slot_list[:]))
+        cast_pair(0)
         nc.vector.tensor_copy(bias_row[:], bias_pool[:].indirect(slot_list[:]))
+        nc.vector.tensor_copy(key_scales[0][:], scale_pool[:].bitcast(U8).indirect(slot_list[:]))
+        nc.scalar.dma_start(key_scales[1][0 : P - SHIFT, :].bitcast(I32), key_scales[0][SHIFT:P, :].bitcast(I32))
 
         for b in range(B):
             for j in range(N // P):
@@ -115,24 +120,25 @@ def tile_attend_lq_score_kernel(tc, qT, k_words, k_scales, kb, offq, offs, out):
                 )
             nc.scalar.copy(bias[b][:], spread[b][:])
 
-        pick_plane(0, 1)
-        halves = key_pairs[:].bitcast(U16).rearrange("p (i o) -> p o i", o=PASSES)
-        for o in range(PASSES):
-            nc.vector.tensor_copy(key_words[o][:].bitcast(U16), halves[:, o, :])
-        pick_plane(0, 2)
-        pick_plane(0, 3)
-        nc.scalar.copy(grouped[0][:], picked[0][:].rearrange("p t q -> p q t"))
-        pick_plane(1, 0)
-        pick_plane(1, 1)
-        nc.scalar.copy(grouped[1][:, :, 0:2], picked[1][:, 0:2, :].rearrange("p t q -> p q t"))
+        nc.vector.tensor_copy(key_pairs[:], word_pool[:].bitcast(U32).indirect(slot_list[:]))
+        pick_pair(0)
+        cast_pair(1)
+        nc.vector.tensor_copy(
+            key_words[:].rearrange("p o w -> p (o w)").bitcast(U16).rearrange("p (o i) -> p o i", o=PASSES),
+            key_pairs[:].bitcast(U16).rearrange("p (i o) -> p o i", o=PASSES),
+        )
+        for t in range(2):
+            nc.vector.tensor_copy(picked[:, t, :], planes[t][:].indirect(query_list[:]))
+        nc.scalar.copy(grouped[1][:, :, 0:2], picked[:].rearrange("p t q -> p q t"))
+        pick_pair(1)
+        nc.vector.tensor_copy(grouped[1][:, :, 2], planes[2][:].indirect(query_list[:]))
         quantize(0, slice(0, QUERIES))
         for b in range(B):
             multiply(0, b)
-        nc.vector.tensor_copy(grouped[1][:, :, 2], planes[PACK + 2][:].indirect(query_list[:]))
         for b in range(B):
             q_cols = slice(b * NQ, (b + 1) * NQ)
             entries = query_list[:, b * NQ // 16 : (b + 1) * NQ // 16]
-            nc.vector.tensor_copy(grouped[1][:, q_cols, 3], planes[PACK + 3][:].indirect(entries))
+            nc.vector.tensor_copy(grouped[1][:, q_cols, 3], planes[3][:].indirect(entries))
         for b in range(B):
             quantize(1, slice(b * NQ, (b + 1) * NQ))
             multiply(1, b)

@@ -31,6 +31,7 @@ def tile_attend_lq_score_kernel(tc, qT, k_words, k_scales, kb, offq, offs, out):
     nc = tc.nc
     with ExitStack() as ctx:
         keep = ctx.enter_context(tc.tile_pool(name="keep", bufs=1))
+        reuse = ctx.enter_context(tc.tile_pool(name="reuse", bufs=1))
         psum = ctx.enter_context(tc.psum_pool(name="psum", bufs=1))
 
         slot_list = keep.tile([P, SLOTS // 16], U16, name="slot_list")
@@ -39,36 +40,45 @@ def tile_attend_lq_score_kernel(tc, qT, k_words, k_scales, kb, offq, offs, out):
         bias_pool = keep.tile([P, T], F32, name="bias_pool", align_bytes=64)
         word_pool = keep.tile([P, T], I32, name="word_pool", align_bytes=64)
         identity = keep.tile([P, P], F32, name="identity", align_bytes=64)
-        plane_pairs = [keep.tile([P, 2, POOL], F32, name="plane_pair%d" % u, align_bytes=64) for u in range(2)]
-        planes = [keep.tile([P, POOL], F32, name="plane%d" % t, align_bytes=64) for t in range(PACK)]
+        plane_pairs = [
+            keep.tile([P, 2, POOL], F32, name="plane_pair0", align_bytes=64),
+            reuse.tile([P, 2, POOL], F32, name="plane_pair1", align_bytes=64, offset=0),
+            keep.tile([P, 2, POOL], F32, name="plane_pair2", align_bytes=64),
+        ]
+        planes = [keep.tile([P, POOL], F32, name="plane%d" % t, align_bytes=64) for t in range(2)]
         q_rows = qT.rearrange("(o p t) c -> o p t c", o=PASSES, t=PACK)
 
-        nc.vector.memset(bias_pool[:], 0.0)
         nc.vector.memset(scale_pool[:], 0)
+        nc.vector.memset(bias_pool[:], 0.0)
         nc.vector.memset(identity[:], 0.0)
         make_identity(nc, identity[:], nomemset=True)
         nc.sync.dma_start(slot_list[:], offs)
         nc.sync.dma_start(query_list[:], offq)
-        nc.sync.dma_start(plane_pairs[0][:], q_rows[0, :, 0:2, :])
-        nc.sync.dma_start(bias_pool[BIAS_ROW : BIAS_ROW + 1, :], kb[0:1, :])
         scale_rows = k_scales.bitcast(I32).rearrange("o (q r) w -> r q o w", r=4)
         for r in range(4):
             nc.sync.dma_start(scale_pool[r:P:SHIFT, :], scale_rows[r])
         nc.sync.dma_start(word_pool[:], k_words[0].rearrange("p t b -> p (t b)").bitcast(I32))
+        nc.sync.dma_start(plane_pairs[0][:], q_rows[0, :, 0:2, :])
+        nc.sync.dma_start(bias_pool[BIAS_ROW : BIAS_ROW + 1, :], kb[0:1, :])
         nc.sync.dma_start(plane_pairs[1][:], q_rows[0, :, 2:4, :])
-        for t in range(PACK):
-            nc.sync.dma_start(planes[t][:], q_rows[1, :, t, :])
+        nc.sync.dma_start(plane_pairs[2][:], q_rows[1, :, 0:2, :])
+        for t in range(2):
+            nc.sync.dma_start(planes[t][:], q_rows[1, :, 2 + t, :])
 
         pair_pool = [keep.tile([P, POOL, 2], BF16, name="pair_pool%d" % u, align_bytes=64) for u in range(2)]
+        first_pair = keep.tile([P, QUERIES], U32, name="first_pair", align_bytes=64)
         picked = keep.tile([P, 2, QUERIES], F32, name="picked", align_bytes=64)
-        grouped = [keep.tile([P, QUERIES, PACK], BF16, name="grouped%d" % o, align_bytes=64) for o in range(PASSES)]
+        grouped = [
+            reuse.tile([P, QUERIES, PACK], BF16, name="grouped0", align_bytes=64, offset=0),
+            keep.tile([P, QUERIES, PACK], BF16, name="grouped1", align_bytes=64),
+        ]
         q_codes = [keep.tile([P, QUERIES], U32, name="q_codes%d" % o, align_bytes=64) for o in range(PASSES)]
         q_scales = [keep.tile([P, QUERIES], U8, name="q_scales%d" % o, align_bytes=64) for o in range(PASSES)]
         key_pairs = keep.tile([P, SLOTS], U32, name="key_pairs", align_bytes=64)
         key_words = keep.tile([P, PASSES, 2 * SLOTS], U8, name="key_words", align_bytes=64)
         key_scales = [keep.tile([P, SLOTS], U8, name="key_scales%d" % o, align_bytes=64) for o in range(PASSES)]
         bias_row = keep.tile([P, SLOTS], F32, name="bias_row", align_bytes=64)
-        bias_cols = keep.tile([P, SLOTS // P], F32, name="bias_cols", align_bytes=64)
+        bias_cols = reuse.tile([P, SLOTS // P], F32, name="bias_cols", align_bytes=64, offset=2 * PACK * QUERIES)
         bias = [keep.tile([P, N], F32, name="bias%d" % b, align_bytes=64) for b in range(B)]
         result = [keep.tile([P, N], F32, name="result%d" % b, align_bytes=64) for b in range(B)]
         turned = [psum.tile([P, N // P, P], F32, name="turned%d" % b) for b in range(B)]
@@ -78,10 +88,9 @@ def tile_attend_lq_score_kernel(tc, qT, k_words, k_scales, kb, offq, offs, out):
         def cast_pair(u):
             nc.scalar.activation(pair_pool[u][:], plane_pairs[u][:].rearrange("p e c -> p c e"), COPY)
 
-        def pick_pair(u):
+        def pick_pair(u, words):
             window = pair_pool[u][:].rearrange("p c e -> p (c e)").bitcast(U32)
-            words = grouped[0][:].rearrange("p q t -> p (q t)").bitcast(U32).rearrange("p (q u) -> p u q", u=2)
-            nc.vector.tensor_copy(words[:, u, :], window.indirect(query_list[:]))
+            nc.vector.tensor_copy(words, window.indirect(query_list[:]))
 
         def quantize(o, cols):
             nc.vector.quantize_mx(
@@ -103,9 +112,17 @@ def tile_attend_lq_score_kernel(tc, qT, k_words, k_scales, kb, offq, offs, out):
             )
 
         cast_pair(0)
-        nc.vector.tensor_copy(bias_row[:], bias_pool[:].indirect(slot_list[:]))
+        cast_pair(1)
         nc.vector.tensor_copy(key_scales[0][:], scale_pool[:].bitcast(U8).indirect(slot_list[:]))
-        nc.scalar.dma_start(key_scales[1][0 : P - SHIFT, :].bitcast(I32), key_scales[0][SHIFT:P, :].bitcast(I32))
+        nc.sync.dma_start(key_scales[1][0 : P - SHIFT, :].bitcast(I32), key_scales[0][SHIFT:P, :].bitcast(I32))
+        nc.vector.tensor_copy(key_pairs[:], word_pool[:].bitcast(U32).indirect(slot_list[:]))
+        nc.vector.tensor_copy(
+            key_words[:].rearrange("p o w -> p (o w)").bitcast(U16).rearrange("p (o i) -> p o i", o=PASSES),
+            key_pairs[:].bitcast(U16).rearrange("p (i o) -> p o i", o=PASSES),
+        )
+        nc.vector.tensor_copy(bias_row[:], bias_pool[:].indirect(slot_list[:]))
+        pick_pair(0, first_pair[:])
+        nc.scalar.copy(grouped[0][:, :, 0:2], first_pair[:].bitcast(BF16).rearrange("p (q e) -> p q e", e=2))
 
         for b in range(B):
             for j in range(N // P):
@@ -120,25 +137,19 @@ def tile_attend_lq_score_kernel(tc, qT, k_words, k_scales, kb, offq, offs, out):
                 )
             nc.scalar.copy(bias[b][:], spread[b][:])
 
-        nc.vector.tensor_copy(key_pairs[:], word_pool[:].bitcast(U32).indirect(slot_list[:]))
-        pick_pair(0)
-        cast_pair(1)
-        nc.vector.tensor_copy(
-            key_words[:].rearrange("p o w -> p (o w)").bitcast(U16).rearrange("p (o i) -> p o i", o=PASSES),
-            key_pairs[:].bitcast(U16).rearrange("p (i o) -> p o i", o=PASSES),
-        )
+        grouped_words = grouped[0][:].rearrange("p q t -> p (q t)").bitcast(U32).rearrange("p (q u) -> p u q", u=2)
+        pick_pair(1, grouped_words[:, 1, :])
         for t in range(2):
-            nc.vector.tensor_copy(picked[:, t, :], planes[t][:].indirect(query_list[:]))
+            nc.vector.tensor_copy(picked[:, t, :], plane_pairs[2][:, t, :].indirect(query_list[:]))
         nc.scalar.copy(grouped[1][:, :, 0:2], picked[:].rearrange("p t q -> p q t"))
-        pick_pair(1)
-        nc.vector.tensor_copy(grouped[1][:, :, 2], planes[2][:].indirect(query_list[:]))
         quantize(0, slice(0, QUERIES))
         for b in range(B):
             multiply(0, b)
+        nc.vector.tensor_copy(grouped[1][:, :, 2], planes[0][:].indirect(query_list[:]))
         for b in range(B):
             q_cols = slice(b * NQ, (b + 1) * NQ)
             entries = query_list[:, b * NQ // 16 : (b + 1) * NQ // 16]
-            nc.vector.tensor_copy(grouped[1][:, q_cols, 3], planes[3][:].indirect(entries))
+            nc.vector.tensor_copy(grouped[1][:, q_cols, 3], planes[1][:].indirect(entries))
         for b in range(B):
             quantize(1, slice(b * NQ, (b + 1) * NQ))
             multiply(1, b)

@@ -43,9 +43,8 @@ def tile_attend_lq_score_kernel(tc, qT, k_words, k_scales, kb, offq, offs, out):
         plane_pairs = [
             keep.tile([P, 2, POOL], F32, name="plane_pair0", align_bytes=64),
             reuse.tile([P, 2, POOL], F32, name="plane_pair1", align_bytes=64, offset=0),
-            keep.tile([P, 2, POOL], F32, name="plane_pair2", align_bytes=64),
         ]
-        planes = [keep.tile([P, POOL], F32, name="plane%d" % t, align_bytes=64) for t in range(2)]
+        planes = [keep.tile([P, POOL], F32, name="plane%d" % t, align_bytes=64) for t in range(PACK)]
         q_rows = qT.rearrange("(o p t) c -> o p t c", o=PASSES, t=PACK)
 
         nc.vector.memset(scale_pool[:], 0)
@@ -54,16 +53,16 @@ def tile_attend_lq_score_kernel(tc, qT, k_words, k_scales, kb, offq, offs, out):
         make_identity(nc, identity[:], nomemset=True)
         nc.sync.dma_start(slot_list[:], offs)
         nc.sync.dma_start(query_list[:], offq)
+        nc.sync.dma_start(planes[2][:], q_rows[1, :, 2, :])
         scale_rows = k_scales.bitcast(I32).rearrange("o (q r) w -> r q o w", r=4)
         for r in range(4):
             nc.sync.dma_start(scale_pool[r:P:SHIFT, :], scale_rows[r])
-        nc.sync.dma_start(word_pool[:], k_words[0].rearrange("p t b -> p (t b)").bitcast(I32))
         nc.sync.dma_start(plane_pairs[0][:], q_rows[0, :, 0:2, :])
         nc.sync.dma_start(bias_pool[BIAS_ROW : BIAS_ROW + 1, :], kb[0:1, :])
+        nc.sync.dma_start(word_pool[:], k_words[0].rearrange("p t b -> p (t b)").bitcast(I32))
         nc.sync.dma_start(plane_pairs[1][:], q_rows[0, :, 2:4, :])
-        nc.sync.dma_start(plane_pairs[2][:], q_rows[1, :, 0:2, :])
-        for t in range(2):
-            nc.sync.dma_start(planes[t][:], q_rows[1, :, 2 + t, :])
+        for t in (0, 1, 3):
+            nc.sync.dma_start(planes[t][:], q_rows[1, :, t, :])
 
         pair_pool = [keep.tile([P, POOL, 2], BF16, name="pair_pool%d" % u, align_bytes=64) for u in range(2)]
         first_pair = keep.tile([P, QUERIES], U32, name="first_pair", align_bytes=64)
@@ -78,8 +77,11 @@ def tile_attend_lq_score_kernel(tc, qT, k_words, k_scales, kb, offq, offs, out):
         key_words = keep.tile([P, PASSES, 2 * SLOTS], U8, name="key_words", align_bytes=64)
         key_scales = [keep.tile([P, SLOTS], U8, name="key_scales%d" % o, align_bytes=64) for o in range(PASSES)]
         bias_row = keep.tile([P, SLOTS], F32, name="bias_row", align_bytes=64)
-        bias_cols = reuse.tile([P, SLOTS // P], F32, name="bias_cols", align_bytes=64, offset=2 * PACK * QUERIES)
-        bias = [keep.tile([P, N], F32, name="bias%d" % b, align_bytes=64) for b in range(B)]
+        bias_cols = keep.tile([P, SLOTS // P], F32, name="bias_cols", align_bytes=64)
+        bias = [
+            reuse.tile([P, N], F32, name="bias%d" % b, align_bytes=64, offset=2 * PACK * QUERIES + 4 * N * b)
+            for b in range(B)
+        ]
         result = [keep.tile([P, N], F32, name="result%d" % b, align_bytes=64) for b in range(B)]
         turned = [psum.tile([P, N // P, P], F32, name="turned%d" % b) for b in range(B)]
         spread = [psum.tile([P, N], F32, name="spread%d" % b) for b in range(B)]
@@ -111,17 +113,18 @@ def tile_attend_lq_score_kernel(tc, qT, k_words, k_scales, kb, offq, offs, out):
                 stop=(o == PASSES - 1),
             )
 
+        nc.vector.tensor_copy(grouped[1][:, :, 2], planes[2][:].indirect(query_list[:]))
         cast_pair(0)
         cast_pair(1)
         nc.vector.tensor_copy(key_scales[0][:], scale_pool[:].bitcast(U8).indirect(slot_list[:]))
         nc.sync.dma_start(key_scales[1][0 : P - SHIFT, :].bitcast(I32), key_scales[0][SHIFT:P, :].bitcast(I32))
+        nc.vector.tensor_copy(bias_row[:], bias_pool[:].indirect(slot_list[:]))
+        pick_pair(0, first_pair[:])
         nc.vector.tensor_copy(key_pairs[:], word_pool[:].bitcast(U32).indirect(slot_list[:]))
         nc.vector.tensor_copy(
             key_words[:].rearrange("p o w -> p (o w)").bitcast(U16).rearrange("p (o i) -> p o i", o=PASSES),
             key_pairs[:].bitcast(U16).rearrange("p (i o) -> p o i", o=PASSES),
         )
-        nc.vector.tensor_copy(bias_row[:], bias_pool[:].indirect(slot_list[:]))
-        pick_pair(0, first_pair[:])
         nc.scalar.copy(grouped[0][:, :, 0:2], first_pair[:].bitcast(BF16).rearrange("p (q e) -> p q e", e=2))
 
         for b in range(B):
@@ -140,16 +143,15 @@ def tile_attend_lq_score_kernel(tc, qT, k_words, k_scales, kb, offq, offs, out):
         grouped_words = grouped[0][:].rearrange("p q t -> p (q t)").bitcast(U32).rearrange("p (q u) -> p u q", u=2)
         pick_pair(1, grouped_words[:, 1, :])
         for t in range(2):
-            nc.vector.tensor_copy(picked[:, t, :], plane_pairs[2][:, t, :].indirect(query_list[:]))
+            nc.vector.tensor_copy(picked[:, t, :], planes[t][:].indirect(query_list[:]))
         nc.scalar.copy(grouped[1][:, :, 0:2], picked[:].rearrange("p t q -> p q t"))
         quantize(0, slice(0, QUERIES))
         for b in range(B):
             multiply(0, b)
-        nc.vector.tensor_copy(grouped[1][:, :, 2], planes[0][:].indirect(query_list[:]))
         for b in range(B):
             q_cols = slice(b * NQ, (b + 1) * NQ)
             entries = query_list[:, b * NQ // 16 : (b + 1) * NQ // 16]
-            nc.vector.tensor_copy(grouped[1][:, q_cols, 3], planes[1][:].indirect(entries))
+            nc.vector.tensor_copy(grouped[1][:, q_cols, 3], planes[3][:].indirect(entries))
         for b in range(B):
             quantize(1, slice(b * NQ, (b + 1) * NQ))
             multiply(1, b)

@@ -53,7 +53,6 @@ def tile_attend_lq_score_kernel(tc, qT, k_words, k_scales, kb, offq, offs, out):
         make_identity(nc, identity[:], nomemset=True)
         nc.sync.dma_start(slot_list[:], offs)
         nc.sync.dma_start(query_list[:], offq)
-        nc.sync.dma_start(planes[2][:], q_rows[1, :, 2, :])
         scale_rows = k_scales.bitcast(I32).rearrange("o (q r) w -> r q o w", r=4)
         for r in range(4):
             nc.sync.dma_start(scale_pool[r:P:SHIFT, :], scale_rows[r])
@@ -61,7 +60,7 @@ def tile_attend_lq_score_kernel(tc, qT, k_words, k_scales, kb, offq, offs, out):
         nc.sync.dma_start(bias_pool[BIAS_ROW : BIAS_ROW + 1, :], kb[0:1, :])
         nc.sync.dma_start(word_pool[:], k_words[0].rearrange("p t b -> p (t b)").bitcast(I32))
         nc.sync.dma_start(plane_pairs[1][:], q_rows[0, :, 2:4, :])
-        for t in (0, 1, 3):
+        for t in range(PACK):
             nc.sync.dma_start(planes[t][:], q_rows[1, :, t, :])
 
         pair_pool = [keep.tile([P, POOL, 2], BF16, name="pair_pool%d" % u, align_bytes=64) for u in range(2)]
@@ -113,7 +112,6 @@ def tile_attend_lq_score_kernel(tc, qT, k_words, k_scales, kb, offq, offs, out):
                 stop=(o == PASSES - 1),
             )
 
-        nc.vector.tensor_copy(grouped[1][:, :, 2], planes[2][:].indirect(query_list[:]))
         cast_pair(0)
         cast_pair(1)
         nc.vector.tensor_copy(key_scales[0][:], scale_pool[:].bitcast(U8).indirect(slot_list[:]))
@@ -148,6 +146,7 @@ def tile_attend_lq_score_kernel(tc, qT, k_words, k_scales, kb, offq, offs, out):
         quantize(0, slice(0, QUERIES))
         for b in range(B):
             multiply(0, b)
+        nc.vector.tensor_copy(grouped[1][:, :, 2], planes[2][:].indirect(query_list[:]))
         for b in range(B):
             q_cols = slice(b * NQ, (b + 1) * NQ)
             entries = query_list[:, b * NQ // 16 : (b + 1) * NQ // 16]

@@ -20,7 +20,7 @@ PACK = 4
 PASSES = D // (P * PACK)
 SLOTS = B * N
 QUERIES = B * NQ
-BIAS_ROW = 8
+BIAS_ROW = P - 1
 SHIFT = 16
 HALF = N // 2
 
@@ -40,36 +40,32 @@ def tile_attend_lq_score_kernel(tc, qT, k_words, k_scales, kb, offq, offs, out):
         bias_pool = keep.tile([P, T], F32, name="bias_pool", align_bytes=64)
         word_pool = keep.tile([P, T], I32, name="word_pool", align_bytes=64)
         identity = keep.tile([P, P], F32, name="identity", align_bytes=64)
-        plane_pairs = [
-            keep.tile([P, 2, POOL], F32, name="plane_pair0", align_bytes=64),
-            reuse.tile([P, 2, POOL], F32, name="plane_pair1", align_bytes=64, offset=0),
-        ]
+        first_planes = [keep.tile([P, POOL], F32, name="first_plane%d" % t, align_bytes=64) for t in range(2)]
+        plane_pair = reuse.tile([P, 2, POOL], F32, name="plane_pair", align_bytes=64, offset=0)
         planes = [keep.tile([P, POOL], F32, name="plane%d" % t, align_bytes=64) for t in range(PACK)]
         q_rows = qT.rearrange("(o p t) c -> o p t c", o=PASSES, t=PACK)
 
         nc.vector.memset(scale_pool[:], 0)
-        nc.vector.memset(bias_pool[:], 0.0)
+        nc.vector.memset(bias_pool[0:BIAS_ROW, :], 0.0)
         nc.vector.memset(identity[:], 0.0)
         make_identity(nc, identity[:], nomemset=True)
         nc.sync.dma_start(slot_list[:], offs)
-        nc.sync.dma_start(query_list[:], offq)
+        nc.sync.dma_start(bias_pool[BIAS_ROW:P, :], kb[0:1, :])
+        nc.sync.dma_start(first_planes[0][:], q_rows[0, :, 0, :])
         scale_rows = k_scales.bitcast(I32).rearrange("o (q r) w -> r q o w", r=4)
         for r in range(4):
             nc.sync.dma_start(scale_pool[r:P:SHIFT, :], scale_rows[r])
-        nc.sync.dma_start(plane_pairs[0][:], q_rows[0, :, 0:2, :])
-        nc.sync.dma_start(bias_pool[BIAS_ROW : BIAS_ROW + 1, :], kb[0:1, :])
+        nc.sync.dma_start(first_planes[1][:], q_rows[0, :, 1, :])
+        nc.sync.dma_start(query_list[:], offq)
         nc.sync.dma_start(word_pool[:], k_words[0].rearrange("p t b -> p (t b)").bitcast(I32))
-        nc.sync.dma_start(plane_pairs[1][:], q_rows[0, :, 2:4, :])
+        nc.sync.dma_start(plane_pair[:], q_rows[0, :, 2:4, :])
         for t in range(PACK):
             nc.sync.dma_start(planes[t][:], q_rows[1, :, t, :])
 
-        pair_pool = [keep.tile([P, POOL, 2], BF16, name="pair_pool%d" % u, align_bytes=64) for u in range(2)]
-        first_pair = keep.tile([P, QUERIES], U32, name="first_pair", align_bytes=64)
+        narrow = [keep.tile([P, POOL], BF16, name="narrow%d" % t, align_bytes=64) for t in range(2)]
+        pair_pool = keep.tile([P, POOL, 2], BF16, name="pair_pool", align_bytes=64)
         picked = keep.tile([P, 2, QUERIES], F32, name="picked", align_bytes=64)
-        grouped = [
-            reuse.tile([P, QUERIES, PACK], BF16, name="grouped0", align_bytes=64, offset=0),
-            keep.tile([P, QUERIES, PACK], BF16, name="grouped1", align_bytes=64),
-        ]
+        grouped = [keep.tile([P, QUERIES, PACK], BF16, name="grouped%d" % o, align_bytes=64) for o in range(PASSES)]
         q_codes = [keep.tile([P, QUERIES], U32, name="q_codes%d" % o, align_bytes=64) for o in range(PASSES)]
         q_scales = [keep.tile([P, QUERIES], U8, name="q_scales%d" % o, align_bytes=64) for o in range(PASSES)]
         key_pairs = keep.tile([P, SLOTS], U32, name="key_pairs", align_bytes=64)
@@ -77,21 +73,11 @@ def tile_attend_lq_score_kernel(tc, qT, k_words, k_scales, kb, offq, offs, out):
         key_scales = [keep.tile([P, SLOTS], U8, name="key_scales%d" % o, align_bytes=64) for o in range(PASSES)]
         bias_row = keep.tile([P, SLOTS], F32, name="bias_row", align_bytes=64)
         bias_cols = keep.tile([P, SLOTS // P], F32, name="bias_cols", align_bytes=64)
-        bias = [
-            reuse.tile([P, N], F32, name="bias%d" % b, align_bytes=64, offset=2 * PACK * QUERIES + 4 * N * b)
-            for b in range(B)
-        ]
+        bias = [reuse.tile([P, N], F32, name="bias%d" % b, align_bytes=64, offset=4 * N * b) for b in range(B)]
         result = [keep.tile([P, N], F32, name="result%d" % b, align_bytes=64) for b in range(B)]
         turned = [psum.tile([P, N // P, P], F32, name="turned%d" % b) for b in range(B)]
         spread = [psum.tile([P, N], F32, name="spread%d" % b) for b in range(B)]
         scores = [psum.tile([P, N], F32, name="scores%d" % b) for b in range(B)]
-
-        def cast_pair(u):
-            nc.scalar.activation(pair_pool[u][:], plane_pairs[u][:].rearrange("p e c -> p c e"), COPY)
-
-        def pick_pair(u, words):
-            window = pair_pool[u][:].rearrange("p c e -> p (c e)").bitcast(U32)
-            nc.vector.tensor_copy(words, window.indirect(query_list[:]))
 
         def quantize(o, cols):
             nc.vector.quantize_mx(
@@ -112,24 +98,25 @@ def tile_attend_lq_score_kernel(tc, qT, k_words, k_scales, kb, offq, offs, out):
                 stop=(o == PASSES - 1),
             )
 
-        cast_pair(0)
-        cast_pair(1)
+        nc.vector.tensor_copy(bias_row[:], bias_pool[:].indirect(slot_list[:]))
         nc.vector.tensor_copy(key_scales[0][:], scale_pool[:].bitcast(U8).indirect(slot_list[:]))
         nc.sync.dma_start(key_scales[1][0 : P - SHIFT, :].bitcast(I32), key_scales[0][SHIFT:P, :].bitcast(I32))
-        nc.vector.tensor_copy(bias_row[:], bias_pool[:].indirect(slot_list[:]))
-        pick_pair(0, first_pair[:])
         nc.vector.tensor_copy(key_pairs[:], word_pool[:].bitcast(U32).indirect(slot_list[:]))
         nc.vector.tensor_copy(
             key_words[:].rearrange("p o w -> p (o w)").bitcast(U16).rearrange("p (o i) -> p o i", o=PASSES),
             key_pairs[:].bitcast(U16).rearrange("p (i o) -> p o i", o=PASSES),
         )
-        nc.scalar.copy(grouped[0][:, :, 0:2], first_pair[:].bitcast(BF16).rearrange("p (q e) -> p q e", e=2))
 
+        for t in range(2):
+            nc.scalar.activation(narrow[t][:], first_planes[t][:], COPY)
+        for t in range(2):
+            nc.scalar.activation(grouped[0][:, :, t], narrow[t][:].indirect(query_list[:]), COPY)
         for b in range(B):
             for j in range(N // P):
                 first = b * N + j * P
                 nc.tensor.transpose(turned[b][:, j, :], bias_row[:, first : first + P], identity[:])
             nc.scalar.copy(bias_cols[:, b * (N // P) : (b + 1) * (N // P)], turned[b][:, :, BIAS_ROW])
+        nc.scalar.activation(pair_pool[:], plane_pair[:].rearrange("p e c -> p c e"), COPY)
         for b in range(B):
             for j in range(N // P):
                 col = b * (N // P) + j
@@ -138,11 +125,12 @@ def tile_attend_lq_score_kernel(tc, qT, k_words, k_scales, kb, offq, offs, out):
                 )
             nc.scalar.copy(bias[b][:], spread[b][:])
 
-        grouped_words = grouped[0][:].rearrange("p q t -> p (q t)").bitcast(U32).rearrange("p (q u) -> p u q", u=2)
-        pick_pair(1, grouped_words[:, 1, :])
         for t in range(2):
             nc.vector.tensor_copy(picked[:, t, :], planes[t][:].indirect(query_list[:]))
         nc.scalar.copy(grouped[1][:, :, 0:2], picked[:].rearrange("p t q -> p q t"))
+        grouped_words = grouped[0][:].rearrange("p q t -> p (q t)").bitcast(U32).rearrange("p (q u) -> p u q", u=2)
+        pair_window = pair_pool[:].rearrange("p c e -> p (c e)").bitcast(U32)
+        nc.vector.tensor_copy(grouped_words[:, 1, :], pair_window.indirect(query_list[:]))
         quantize(0, slice(0, QUERIES))
         for b in range(B):
             multiply(0, b)

@@ -32,6 +32,7 @@ def tile_attend_lq_score_kernel(tc, qT, k_words, k_scales, kb, offq, offs, out):
     with ExitStack() as ctx:
         keep = ctx.enter_context(tc.tile_pool(name="keep", bufs=1))
         reuse = ctx.enter_context(tc.tile_pool(name="reuse", bufs=1))
+        late = ctx.enter_context(tc.tile_pool(name="late", bufs=1))
         psum = ctx.enter_context(tc.psum_pool(name="psum", bufs=1))
 
         slot_list = keep.tile([P, SLOTS // 16], U16, name="slot_list")
@@ -41,8 +42,8 @@ def tile_attend_lq_score_kernel(tc, qT, k_words, k_scales, kb, offq, offs, out):
         word_pool = keep.tile([P, T], I32, name="word_pool", align_bytes=64)
         identity = keep.tile([P, P], F32, name="identity", align_bytes=64)
         first_planes = [keep.tile([P, POOL], F32, name="first_plane%d" % t, align_bytes=64) for t in range(2)]
-        plane_pair = reuse.tile([P, 2, POOL], F32, name="plane_pair", align_bytes=64, offset=0)
-        planes = [keep.tile([P, POOL], F32, name="plane%d" % t, align_bytes=64) for t in range(PACK)]
+        plane_pair = keep.tile([P, 2, POOL], F32, name="plane_pair", align_bytes=64)
+        planes = [reuse.tile([P, POOL], F32, name="plane%d" % t, align_bytes=64, offset=4 * POOL * t) for t in range(PACK)]
         q_rows = qT.rearrange("(o p t) c -> o p t c", o=PASSES, t=PACK)
 
         nc.vector.memset(scale_pool[:], 0)
@@ -51,29 +52,39 @@ def tile_attend_lq_score_kernel(tc, qT, k_words, k_scales, kb, offq, offs, out):
         make_identity(nc, identity[:], nomemset=True)
         nc.sync.dma_start(slot_list[:], offs)
         nc.sync.dma_start(bias_pool[BIAS_ROW:P, :], kb[0:1, :])
-        nc.sync.dma_start(first_planes[0][:], q_rows[0, :, 0, :])
+        nc.sync.dma_start(plane_pair[:], q_rows[0, :, 2:4, :])
         scale_rows = k_scales.bitcast(I32).rearrange("o (q r) w -> r q o w", r=4)
         for r in range(4):
             nc.sync.dma_start(scale_pool[r:P:SHIFT, :], scale_rows[r])
-        nc.sync.dma_start(first_planes[1][:], q_rows[0, :, 1, :])
         nc.sync.dma_start(query_list[:], offq)
         nc.sync.dma_start(word_pool[:], k_words[0].rearrange("p t b -> p (t b)").bitcast(I32))
-        nc.sync.dma_start(plane_pair[:], q_rows[0, :, 2:4, :])
+        for t in range(2):
+            nc.sync.dma_start(first_planes[t][:], q_rows[0, :, t, :])
         for t in range(PACK):
             nc.sync.dma_start(planes[t][:], q_rows[1, :, t, :])
 
-        narrow = [keep.tile([P, POOL], BF16, name="narrow%d" % t, align_bytes=64) for t in range(2)]
-        pair_pool = keep.tile([P, POOL, 2], BF16, name="pair_pool", align_bytes=64)
+        narrow = [
+            keep.tile([P, POOL], BF16, name="narrow0", align_bytes=64),
+            late.tile([P, POOL], BF16, name="narrow1", align_bytes=64, offset=0),
+        ]
+        pair_pool = reuse.tile([P, POOL, 2], BF16, name="pair_pool", align_bytes=64, offset=4 * POOL * PACK)
         picked = keep.tile([P, 2, QUERIES], F32, name="picked", align_bytes=64)
         grouped = [keep.tile([P, QUERIES, PACK], BF16, name="grouped%d" % o, align_bytes=64) for o in range(PASSES)]
-        q_codes = [keep.tile([P, QUERIES], U32, name="q_codes%d" % o, align_bytes=64) for o in range(PASSES)]
+        q_codes = [
+            reuse.tile([P, QUERIES], U32, name="q_codes0", align_bytes=64, offset=4 * POOL),
+            keep.tile([P, QUERIES], U32, name="q_codes1", align_bytes=64),
+        ]
         q_scales = [keep.tile([P, QUERIES], U8, name="q_scales%d" % o, align_bytes=64) for o in range(PASSES)]
-        key_pairs = keep.tile([P, SLOTS], U32, name="key_pairs", align_bytes=64)
+        key_pairs = reuse.tile([P, SLOTS], U32, name="key_pairs", align_bytes=64, offset=4 * POOL * PACK)
         key_words = keep.tile([P, PASSES, 2 * SLOTS], U8, name="key_words", align_bytes=64)
-        key_scales = [keep.tile([P, SLOTS], U8, name="key_scales%d" % o, align_bytes=64) for o in range(PASSES)]
+        key_scales = [
+            keep.tile([P, SLOTS], U8, name="key_scales0", align_bytes=64),
+            late.tile([P, SLOTS], U8, name="key_scales1", align_bytes=64, offset=0),
+        ]
         bias_row = keep.tile([P, SLOTS], F32, name="bias_row", align_bytes=64)
         bias_cols = keep.tile([P, SLOTS // P], F32, name="bias_cols", align_bytes=64)
-        bias = [reuse.tile([P, N], F32, name="bias%d" % b, align_bytes=64, offset=4 * N * b) for b in range(B)]
+        bias_rows = late.tile([P, B, N], F32, name="bias_rows", align_bytes=64, offset=SLOTS)
+        bias = [bias_rows[:, b, :] for b in range(B)]
         result = [keep.tile([P, N], F32, name="result%d" % b, align_bytes=64) for b in range(B)]
         turned = [psum.tile([P, N // P, P], F32, name="turned%d" % b) for b in range(B)]
         spread = [psum.tile([P, N], F32, name="spread%d" % b) for b in range(B)]
@@ -98,39 +109,40 @@ def tile_attend_lq_score_kernel(tc, qT, k_words, k_scales, kb, offq, offs, out):
                 stop=(o == PASSES - 1),
             )
 
+        nc.scalar.activation(pair_pool[:], plane_pair[:].rearrange("p e c -> p c e"), COPY)
         nc.vector.tensor_copy(bias_row[:], bias_pool[:].indirect(slot_list[:]))
         nc.vector.tensor_copy(key_scales[0][:], scale_pool[:].bitcast(U8).indirect(slot_list[:]))
-        nc.sync.dma_start(key_scales[1][0 : P - SHIFT, :].bitcast(I32), key_scales[0][SHIFT:P, :].bitcast(I32))
+        grouped_words = grouped[0][:].rearrange("p q t -> p (q t)").bitcast(U32).rearrange("p (q u) -> p u q", u=2)
+        pair_window = pair_pool[:].rearrange("p c e -> p (c e)").bitcast(U32)
+        nc.vector.tensor_copy(grouped_words[:, 1, :], pair_window.indirect(query_list[:]))
         nc.vector.tensor_copy(key_pairs[:], word_pool[:].bitcast(U32).indirect(slot_list[:]))
         nc.vector.tensor_copy(
             key_words[:].rearrange("p o w -> p (o w)").bitcast(U16).rearrange("p (o i) -> p o i", o=PASSES),
             key_pairs[:].bitcast(U16).rearrange("p (i o) -> p o i", o=PASSES),
         )
 
-        for t in range(2):
-            nc.scalar.activation(narrow[t][:], first_planes[t][:], COPY)
-        for t in range(2):
-            nc.scalar.activation(grouped[0][:, :, t], narrow[t][:].indirect(query_list[:]), COPY)
         for b in range(B):
             for j in range(N // P):
                 first = b * N + j * P
                 nc.tensor.transpose(turned[b][:, j, :], bias_row[:, first : first + P], identity[:])
             nc.scalar.copy(bias_cols[:, b * (N // P) : (b + 1) * (N // P)], turned[b][:, :, BIAS_ROW])
-        nc.scalar.activation(pair_pool[:], plane_pair[:].rearrange("p e c -> p c e"), COPY)
+        for t in range(2):
+            nc.scalar.activation(narrow[t][:], first_planes[t][:], COPY)
+        for t in range(2):
+            nc.scalar.activation(grouped[0][:, :, t], narrow[t][:].indirect(query_list[:]), COPY)
+        for r in range(4):
+            nc.scalar.dma_start(key_scales[1][r:P:32, :].bitcast(I32), key_scales[0][SHIFT + r : P : 32, :].bitcast(I32))
+
+        for t in range(2):
+            nc.vector.tensor_copy(picked[:, t, :], planes[t][:].indirect(query_list[:]))
+        nc.scalar.copy(grouped[1][:, :, 0:2], picked[:].rearrange("p t q -> p q t"))
         for b in range(B):
             for j in range(N // P):
                 col = b * (N // P) + j
                 nc.tensor.transpose(
                     spread[b][:, j * P : (j + 1) * P], bias_cols[:, col : col + 1].to_broadcast([P, P]), identity[:]
                 )
-            nc.scalar.copy(bias[b][:], spread[b][:])
-
-        for t in range(2):
-            nc.vector.tensor_copy(picked[:, t, :], planes[t][:].indirect(query_list[:]))
-        nc.scalar.copy(grouped[1][:, :, 0:2], picked[:].rearrange("p t q -> p q t"))
-        grouped_words = grouped[0][:].rearrange("p q t -> p (q t)").bitcast(U32).rearrange("p (q u) -> p u q", u=2)
-        pair_window = pair_pool[:].rearrange("p c e -> p (c e)").bitcast(U32)
-        nc.vector.tensor_copy(grouped_words[:, 1, :], pair_window.indirect(query_list[:]))
+            nc.scalar.copy(bias[b], spread[b][:])
         quantize(0, slice(0, QUERIES))
         for b in range(B):
             multiply(0, b)

@@ -23,6 +23,7 @@ QUERIES = B * NQ
 BIAS_ROW = P - 1
 SHIFT = 16
 HALF = N // 2
+BANK = 2048
 
 FLOPS = 2 * B * NQ * N * D
 
@@ -41,7 +42,10 @@ def tile_attend_lq_score_kernel(tc, qT, k_words, k_scales, kb, offq, offs, out):
         bias_pool = keep.tile([P, T], F32, name="bias_pool", align_bytes=64)
         word_pool = keep.tile([P, T], I32, name="word_pool", align_bytes=64)
         identity = keep.tile([P, P], F32, name="identity", align_bytes=64)
-        first_planes = [keep.tile([P, POOL], F32, name="first_plane%d" % t, align_bytes=64) for t in range(2)]
+        first_planes = [
+            reuse.tile([P, POOL], F32, name="first_plane0", align_bytes=64, offset=4 * POOL * (PACK + 1)),
+            keep.tile([P, POOL], F32, name="first_plane1", align_bytes=64),
+        ]
         plane_pair = keep.tile([P, 2, POOL], F32, name="plane_pair", align_bytes=64)
         planes = [reuse.tile([P, POOL], F32, name="plane%d" % t, align_bytes=64, offset=4 * POOL * t) for t in range(PACK)]
         q_rows = qT.rearrange("(o p t) c -> o p t c", o=PASSES, t=PACK)
@@ -51,15 +55,15 @@ def tile_attend_lq_score_kernel(tc, qT, k_words, k_scales, kb, offq, offs, out):
         nc.vector.memset(identity[:], 0.0)
         make_identity(nc, identity[:], nomemset=True)
         nc.sync.dma_start(slot_list[:], offs)
-        nc.sync.dma_start(bias_pool[BIAS_ROW:P, :], kb[0:1, :])
+        nc.scalar.dma_start(bias_pool[BIAS_ROW:P, :], kb[0:1, :])
         nc.sync.dma_start(plane_pair[:], q_rows[0, :, 2:4, :])
         scale_rows = k_scales.bitcast(I32).rearrange("o (q r) w -> r q o w", r=4)
         for r in range(4):
             nc.sync.dma_start(scale_pool[r:P:SHIFT, :], scale_rows[r])
         nc.sync.dma_start(query_list[:], offq)
+        nc.sync.dma_start(first_planes[0][:], q_rows[0, :, 0, :])
         nc.sync.dma_start(word_pool[:], k_words[0].rearrange("p t b -> p (t b)").bitcast(I32))
-        for t in range(2):
-            nc.sync.dma_start(first_planes[t][:], q_rows[0, :, t, :])
+        nc.sync.dma_start(first_planes[1][:], q_rows[0, :, 1, :])
         for t in range(PACK):
             nc.sync.dma_start(planes[t][:], q_rows[1, :, t, :])
 
@@ -79,16 +83,16 @@ def tile_attend_lq_score_kernel(tc, qT, k_words, k_scales, kb, offq, offs, out):
         key_words = keep.tile([P, PASSES, 2 * SLOTS], U8, name="key_words", align_bytes=64)
         key_scales = [
             keep.tile([P, SLOTS], U8, name="key_scales0", align_bytes=64),
-            late.tile([P, SLOTS], U8, name="key_scales1", align_bytes=64, offset=0),
+            keep.tile([P, SLOTS], U8, name="key_scales1", align_bytes=64),
         ]
         bias_row = keep.tile([P, SLOTS], F32, name="bias_row", align_bytes=64)
-        bias_cols = keep.tile([P, SLOTS // P], F32, name="bias_cols", align_bytes=64)
+        bias_cols = reuse.tile([P, SLOTS // P], F32, name="bias_cols", align_bytes=64, offset=4 * POOL * (PACK + 1))
         bias_rows = late.tile([P, B, N], F32, name="bias_rows", align_bytes=64, offset=SLOTS)
         bias = [bias_rows[:, b, :] for b in range(B)]
         result = [keep.tile([P, N], F32, name="result%d" % b, align_bytes=64) for b in range(B)]
-        turned = [psum.tile([P, N // P, P], F32, name="turned%d" % b) for b in range(B)]
-        spread = [psum.tile([P, N], F32, name="spread%d" % b) for b in range(B)]
-        scores = [psum.tile([P, N], F32, name="scores%d" % b) for b in range(B)]
+        turned = [psum.tile([P, N // P, P], F32, name="turned%d" % b, offset=BANK * (4 + b)) for b in range(B)]
+        spread = [psum.tile([P, N], F32, name="spread%d" % b, offset=BANK * (6 + b)) for b in range(B)]
+        scores = [psum.tile([P, P], F32, name="scores%d" % g, offset=BANK * g) for g in range(SLOTS // P)]
 
         def quantize(o, cols):
             nc.vector.quantize_mx(
@@ -99,15 +103,16 @@ def tile_attend_lq_score_kernel(tc, qT, k_words, k_scales, kb, offq, offs, out):
 
         def multiply(o, b):
             q_cols = slice(b * NQ, (b + 1) * NQ)
-            nc.tensor.matmul_mx(
-                out=scores[b][:],
-                lhsT=q_codes[o][:, q_cols].bitcast(FP8X4),
-                lhsT_scale=q_scales[o][:, q_cols],
-                rhs=key_words[:, o, 2 * b * N : 2 * (b + 1) * N].bitcast(FP4X4),
-                rhs_scale=key_scales[o][:, b * N : (b + 1) * N],
-                start=(o == 0),
-                stop=(o == PASSES - 1),
-            )
+            for g in range(b * N // P, (b + 1) * N // P):
+                nc.tensor.matmul_mx(
+                    out=scores[g][:],
+                    lhsT=q_codes[o][:, q_cols].bitcast(FP8X4),
+                    lhsT_scale=q_scales[o][:, q_cols],
+                    rhs=key_words[:, o, 2 * g * P : 2 * (g + 1) * P].bitcast(FP4X4),
+                    rhs_scale=key_scales[o][:, g * P : (g + 1) * P],
+                    start=(o == 0),
+                    stop=(o == PASSES - 1),
+                )
 
         nc.scalar.activation(pair_pool[:], plane_pair[:].rearrange("p e c -> p c e"), COPY)
         nc.vector.tensor_copy(bias_row[:], bias_pool[:].indirect(slot_list[:]))
@@ -121,17 +126,17 @@ def tile_attend_lq_score_kernel(tc, qT, k_words, k_scales, kb, offq, offs, out):
             key_pairs[:].bitcast(U16).rearrange("p (i o) -> p o i", o=PASSES),
         )
 
+        nc.scalar.activation(narrow[0][:], first_planes[0][:], COPY)
         for b in range(B):
             for j in range(N // P):
                 first = b * N + j * P
                 nc.tensor.transpose(turned[b][:, j, :], bias_row[:, first : first + P], identity[:])
             nc.scalar.copy(bias_cols[:, b * (N // P) : (b + 1) * (N // P)], turned[b][:, :, BIAS_ROW])
-        for t in range(2):
-            nc.scalar.activation(narrow[t][:], first_planes[t][:], COPY)
-        for t in range(2):
-            nc.scalar.activation(grouped[0][:, :, t], narrow[t][:].indirect(query_list[:]), COPY)
+        nc.scalar.activation(grouped[0][:, :, 0], narrow[0][:].indirect(query_list[:]), COPY)
+        nc.scalar.activation(narrow[1][:], first_planes[1][:], COPY)
+        nc.scalar.activation(grouped[0][:, :, 1], narrow[1][:].indirect(query_list[:]), COPY)
         for r in range(4):
-            nc.scalar.dma_start(key_scales[1][r:P:32, :].bitcast(I32), key_scales[0][SHIFT + r : P : 32, :].bitcast(I32))
+            nc.sync.dma_start(key_scales[1][r:P:32, :].bitcast(I32), key_scales[0][SHIFT + r : P : 32, :].bitcast(I32))
 
         for t in range(2):
             nc.vector.tensor_copy(picked[:, t, :], planes[t][:].indirect(query_list[:]))
@@ -157,6 +162,8 @@ def tile_attend_lq_score_kernel(tc, qT, k_words, k_scales, kb, offq, offs, out):
         for b in range(B):
             for h in range(2):
                 cols = slice(h * HALF, (h + 1) * HALF)
-                nc.vector.tensor_tensor(result[b][:, cols], scores[b][:, cols], bias[b][:, cols], ADD)
+                for j in range(2 * h, 2 * h + 2):
+                    part = slice(j * P, (j + 1) * P)
+                    nc.vector.tensor_tensor(result[b][:, part], scores[b * N // P + j][:], bias[b][:, part], ADD)
                 queue = nc.sync if h == 0 else nc.scalar
                 queue.dma_start(out[b, :, cols], result[b][:, cols])

@@ -43,11 +43,11 @@ def tile_attend_lq_score_kernel(tc, qT, k_words, k_scales, kb, offq, offs, out):
         word_pool = keep.tile([P, T], I32, name="word_pool", align_bytes=64)
         identity = keep.tile([P, P], F32, name="identity", align_bytes=64)
         first_planes = [
-            reuse.tile([P, POOL], F32, name="first_plane0", align_bytes=64, offset=4 * POOL * (PACK + 1)),
+            reuse.tile([P, POOL], F32, name="first_plane0", align_bytes=64, offset=0),
             keep.tile([P, POOL], F32, name="first_plane1", align_bytes=64),
         ]
         plane_pair = keep.tile([P, 2, POOL], F32, name="plane_pair", align_bytes=64)
-        planes = [reuse.tile([P, POOL], F32, name="plane%d" % t, align_bytes=64, offset=4 * POOL * t) for t in range(PACK)]
+        planes = [keep.tile([P, POOL], F32, name="plane%d" % t, align_bytes=64) for t in range(PACK)]
         q_rows = qT.rearrange("(o p t) c -> o p t c", o=PASSES, t=PACK)
 
         nc.vector.memset(scale_pool[:], 0)
@@ -71,22 +71,19 @@ def tile_attend_lq_score_kernel(tc, qT, k_words, k_scales, kb, offq, offs, out):
             keep.tile([P, POOL], BF16, name="narrow0", align_bytes=64),
             late.tile([P, POOL], BF16, name="narrow1", align_bytes=64, offset=0),
         ]
-        pair_pool = reuse.tile([P, POOL, 2], BF16, name="pair_pool", align_bytes=64, offset=4 * POOL * PACK)
+        pair_pool = keep.tile([P, POOL, 2], BF16, name="pair_pool", align_bytes=64)
         picked = keep.tile([P, 2, QUERIES], F32, name="picked", align_bytes=64)
         grouped = [keep.tile([P, QUERIES, PACK], BF16, name="grouped%d" % o, align_bytes=64) for o in range(PASSES)]
-        q_codes = [
-            reuse.tile([P, QUERIES], U32, name="q_codes0", align_bytes=64, offset=4 * POOL),
-            keep.tile([P, QUERIES], U32, name="q_codes1", align_bytes=64),
-        ]
+        q_codes = [keep.tile([P, QUERIES], U32, name="q_codes%d" % o, align_bytes=64) for o in range(PASSES)]
         q_scales = [keep.tile([P, QUERIES], U8, name="q_scales%d" % o, align_bytes=64) for o in range(PASSES)]
-        key_pairs = reuse.tile([P, SLOTS], U32, name="key_pairs", align_bytes=64, offset=4 * POOL * PACK)
-        key_words = keep.tile([P, PASSES, 2 * SLOTS], U8, name="key_words", align_bytes=64)
+        key_pairs = [keep.tile([P, N], U32, name="key_pairs%d" % b, align_bytes=64) for b in range(B)]
+        key_words = [keep.tile([P, PASSES, 2 * N], U8, name="key_words%d" % b, align_bytes=64) for b in range(B)]
         key_scales = [
             keep.tile([P, SLOTS], U8, name="key_scales0", align_bytes=64),
             keep.tile([P, SLOTS], U8, name="key_scales1", align_bytes=64),
         ]
         bias_row = keep.tile([P, SLOTS], F32, name="bias_row", align_bytes=64)
-        bias_cols = reuse.tile([P, SLOTS // P], F32, name="bias_cols", align_bytes=64, offset=4 * POOL * (PACK + 1))
+        bias_cols = reuse.tile([P, SLOTS // P], F32, name="bias_cols", align_bytes=64, offset=0)
         bias_rows = late.tile([P, B, N], F32, name="bias_rows", align_bytes=64, offset=SLOTS)
         bias = [bias_rows[:, b, :] for b in range(B)]
         result = [keep.tile([P, N], F32, name="result%d" % b, align_bytes=64) for b in range(B)]
@@ -108,7 +105,7 @@ def tile_attend_lq_score_kernel(tc, qT, k_words, k_scales, kb, offq, offs, out):
                     out=scores[g][:],
                     lhsT=q_codes[o][:, q_cols].bitcast(FP8X4),
                     lhsT_scale=q_scales[o][:, q_cols],
-                    rhs=key_words[:, o, 2 * g * P : 2 * (g + 1) * P].bitcast(FP4X4),
+                    rhs=key_words[b][:, o, 2 * (g * P - b * N) : 2 * ((g + 1) * P - b * N)].bitcast(FP4X4),
                     rhs_scale=key_scales[o][:, g * P : (g + 1) * P],
                     start=(o == 0),
                     stop=(o == PASSES - 1),
@@ -120,11 +117,14 @@ def tile_attend_lq_score_kernel(tc, qT, k_words, k_scales, kb, offq, offs, out):
         grouped_words = grouped[0][:].rearrange("p q t -> p (q t)").bitcast(U32).rearrange("p (q u) -> p u q", u=2)
         pair_window = pair_pool[:].rearrange("p c e -> p (c e)").bitcast(U32)
         nc.vector.tensor_copy(grouped_words[:, 1, :], pair_window.indirect(query_list[:]))
-        nc.vector.tensor_copy(key_pairs[:], word_pool[:].bitcast(U32).indirect(slot_list[:]))
-        nc.vector.tensor_copy(
-            key_words[:].rearrange("p o w -> p (o w)").bitcast(U16).rearrange("p (o i) -> p o i", o=PASSES),
-            key_pairs[:].bitcast(U16).rearrange("p (i o) -> p o i", o=PASSES),
-        )
+        for b in range(B):
+            entries = slot_list[:, b * N // 16 : (b + 1) * N // 16]
+            nc.vector.tensor_copy(key_pairs[b][:], word_pool[:].bitcast(U32).indirect(entries))
+        for b in range(B):
+            nc.vector.tensor_copy(
+                key_words[b][:].rearrange("p o w -> p (o w)").bitcast(U16).rearrange("p (o i) -> p o i", o=PASSES),
+                key_pairs[b][:].bitcast(U16).rearrange("p (i o) -> p o i", o=PASSES),
+            )
 
         nc.scalar.activation(narrow[0][:], first_planes[0][:], COPY)
         for b in range(B):

@@ -47,7 +47,7 @@ def tile_attend_lq_score_kernel(tc, qT, k_words, k_scales, kb, offq, offs, out):
             keep.tile([P, POOL], F32, name="first_plane1", align_bytes=64),
         ]
         plane_pair = keep.tile([P, 2, POOL], F32, name="plane_pair", align_bytes=64)
-        planes = [keep.tile([P, POOL], F32, name="plane%d" % t, align_bytes=64) for t in range(PACK)]
+        planes = [reuse.tile([P, POOL], F32, name="plane%d" % t, align_bytes=64, offset=4 * POOL * (t + 1)) for t in range(PACK)]
         q_rows = qT.rearrange("(o p t) c -> o p t c", o=PASSES, t=PACK)
 
         nc.vector.memset(scale_pool[:], 0)
@@ -77,7 +77,12 @@ def tile_attend_lq_score_kernel(tc, qT, k_words, k_scales, kb, offq, offs, out):
         q_codes = [keep.tile([P, QUERIES], U32, name="q_codes%d" % o, align_bytes=64) for o in range(PASSES)]
         q_scales = [keep.tile([P, QUERIES], U8, name="q_scales%d" % o, align_bytes=64) for o in range(PASSES)]
         key_pairs = [keep.tile([P, N], U32, name="key_pairs%d" % b, align_bytes=64) for b in range(B)]
-        key_words = [keep.tile([P, PASSES, 2 * N], U8, name="key_words%d" % b, align_bytes=64) for b in range(B)]
+        first_words = keep.tile([P, PASSES, 2 * N], U8, name="first_words", align_bytes=64)
+        second_words = [
+            keep.tile([P, 2 * N], U8, name="second_words0", align_bytes=64),
+            reuse.tile([P, 2 * N], U8, name="second_words1", align_bytes=64, offset=4 * POOL * PACK),
+        ]
+        key_words = [[first_words[:, o, :] for o in range(PASSES)], [second_words[o][:] for o in range(PASSES)]]
         key_scales = [
             keep.tile([P, SLOTS], U8, name="key_scales0", align_bytes=64),
             keep.tile([P, SLOTS], U8, name="key_scales1", align_bytes=64),
@@ -105,7 +110,7 @@ def tile_attend_lq_score_kernel(tc, qT, k_words, k_scales, kb, offq, offs, out):
                     out=scores[g][:],
                     lhsT=q_codes[o][:, q_cols].bitcast(FP8X4),
                     lhsT_scale=q_scales[o][:, q_cols],
-                    rhs=key_words[b][:, o, 2 * (g * P - b * N) : 2 * ((g + 1) * P - b * N)].bitcast(FP4X4),
+                    rhs=key_words[b][o][:, 2 * (g * P - b * N) : 2 * ((g + 1) * P - b * N)].bitcast(FP4X4),
                     rhs_scale=key_scales[o][:, g * P : (g + 1) * P],
                     start=(o == 0),
                     stop=(o == PASSES - 1),
@@ -120,11 +125,11 @@ def tile_attend_lq_score_kernel(tc, qT, k_words, k_scales, kb, offq, offs, out):
         for b in range(B):
             entries = slot_list[:, b * N // 16 : (b + 1) * N // 16]
             nc.vector.tensor_copy(key_pairs[b][:], word_pool[:].bitcast(U32).indirect(entries))
-        for b in range(B):
-            nc.vector.tensor_copy(
-                key_words[b][:].rearrange("p o w -> p (o w)").bitcast(U16).rearrange("p (o i) -> p o i", o=PASSES),
-                key_pairs[b][:].bitcast(U16).rearrange("p (i o) -> p o i", o=PASSES),
-            )
+        halves = [key_pairs[b][:].bitcast(U16).rearrange("p (i o) -> p o i", o=PASSES) for b in range(B)]
+        nc.vector.tensor_copy(
+            first_words[:].rearrange("p o w -> p (o w)").bitcast(U16).rearrange("p (o i) -> p o i", o=PASSES), halves[0]
+        )
+        nc.vector.tensor_copy(second_words[0][:].bitcast(U16), halves[1][:, 0, :])
 
         nc.scalar.activation(narrow[0][:], first_planes[0][:], COPY)
         for b in range(B):
@@ -158,6 +163,8 @@ def tile_attend_lq_score_kernel(tc, qT, k_words, k_scales, kb, offq, offs, out):
             nc.vector.tensor_copy(grouped[1][:, q_cols, 3], planes[3][:].indirect(entries))
         for b in range(B):
             quantize(1, slice(b * NQ, (b + 1) * NQ))
+        nc.vector.tensor_copy(second_words[1][:].bitcast(U16), halves[1][:, 1, :])
+        for b in range(B):
             multiply(1, b)
         for b in range(B):
             for h in range(2):

@@ -24,6 +24,7 @@ BIAS_ROW = P - 1
 SHIFT = 16
 HALF = N // 2
 BANK = 2048
+APART = 24 * 1024
 
 FLOPS = 2 * B * NQ * N * D
 
@@ -40,14 +41,14 @@ def tile_attend_lq_score_kernel(tc, qT, k_words, k_scales, kb, offq, offs, out):
         query_list = keep.tile([P, QUERIES // 16], U16, name="query_list")
         scale_pool = keep.tile([P, T // 4], I32, name="scale_pool", align_bytes=64)
         bias_pool = keep.tile([P, T], F32, name="bias_pool", align_bytes=64)
-        word_pool = keep.tile([P, T], I32, name="word_pool", align_bytes=64)
+        word_pool = reuse.tile([P, T], I32, name="word_pool", align_bytes=1024, offset=2 * APART)
         identity = keep.tile([P, P], F32, name="identity", align_bytes=64)
         first_planes = [
-            reuse.tile([P, POOL], F32, name="first_plane0", align_bytes=64, offset=0),
-            keep.tile([P, POOL], F32, name="first_plane1", align_bytes=64),
+            reuse.tile([P, POOL], F32, name="first_plane0", align_bytes=1024, offset=APART),
+            reuse.tile([P, POOL], F32, name="first_plane1", align_bytes=1024, offset=3 * APART),
         ]
-        plane_pair = keep.tile([P, 2, POOL], F32, name="plane_pair", align_bytes=64)
-        planes = [reuse.tile([P, POOL], F32, name="plane%d" % t, align_bytes=64, offset=4 * POOL * (t + 1)) for t in range(PACK)]
+        plane_pair = reuse.tile([P, 2, POOL], F32, name="plane_pair", align_bytes=1024, offset=12 * 1024)
+        planes = [reuse.tile([P, POOL], F32, name="plane%d" % t, align_bytes=1024, offset=APART * (t + 4)) for t in range(PACK)]
         q_rows = qT.rearrange("(o p t) c -> o p t c", o=PASSES, t=PACK)
 
         nc.vector.memset(scale_pool[:], 0)
@@ -80,7 +81,7 @@ def tile_attend_lq_score_kernel(tc, qT, k_words, k_scales, kb, offq, offs, out):
         first_words = keep.tile([P, PASSES, 2 * N], U8, name="first_words", align_bytes=64)
         second_words = [
             keep.tile([P, 2 * N], U8, name="second_words0", align_bytes=64),
-            reuse.tile([P, 2 * N], U8, name="second_words1", align_bytes=64, offset=4 * POOL * PACK),
+            reuse.tile([P, 2 * N], U8, name="second_words1", align_bytes=64, offset=APART * (PACK + 3)),
         ]
         key_words = [[first_words[:, o, :] for o in range(PASSES)], [second_words[o][:] for o in range(PASSES)]]
         key_scales = [
@@ -88,7 +89,7 @@ def tile_attend_lq_score_kernel(tc, qT, k_words, k_scales, kb, offq, offs, out):
             keep.tile([P, SLOTS], U8, name="key_scales1", align_bytes=64),
         ]
         bias_row = keep.tile([P, SLOTS], F32, name="bias_row", align_bytes=64)
-        bias_cols = reuse.tile([P, SLOTS // P], F32, name="bias_cols", align_bytes=64, offset=0)
+        bias_cols = reuse.tile([P, SLOTS // P], F32, name="bias_cols", align_bytes=64, offset=APART)
         bias_rows = late.tile([P, B, N], F32, name="bias_rows", align_bytes=64, offset=SLOTS)
         bias = [bias_rows[:, b, :] for b in range(B)]
         result = [keep.tile([P, N], F32, name="result%d" % b, align_bytes=64) for b in range(B)]

@@ -21,7 +21,6 @@ PASSES = D // (P * PACK)
 SLOTS = B * N
 QUERIES = B * NQ
 BIAS_ROW = P - 1
-SHIFT = 16
 HALF = N // 2
 BANK = 2048
 APART = 24 * 1024
@@ -58,9 +57,7 @@ def tile_attend_lq_score_kernel(tc, qT, k_words, k_scales, kb, offq, offs, out):
         nc.sync.dma_start(slot_list[:], offs)
         nc.scalar.dma_start(bias_pool[BIAS_ROW:P, :], kb[0:1, :])
         nc.sync.dma_start(plane_pair[:], q_rows[0, :, 2:4, :])
-        scale_rows = k_scales.bitcast(I32).rearrange("o (q r) w -> r q o w", r=4)
-        for r in range(4):
-            nc.sync.dma_start(scale_pool[r:P:SHIFT, :], scale_rows[r])
+        nc.sync.dma_start(scale_pool[0:P:4, :], k_scales.bitcast(I32).rearrange("o f w -> f o w"))
         nc.sync.dma_start(query_list[:], offq)
         nc.sync.dma_start(first_planes[0][:], q_rows[0, :, 0, :])
         nc.sync.dma_start(word_pool[:], k_words[0].rearrange("p t b -> p (t b)").bitcast(I32))
@@ -84,10 +81,9 @@ def tile_attend_lq_score_kernel(tc, qT, k_words, k_scales, kb, offq, offs, out):
             reuse.tile([P, 2 * N], U8, name="second_words1", align_bytes=64, offset=APART * (PACK + 3)),
         ]
         key_words = [[first_words[:, o, :] for o in range(PASSES)], [second_words[o][:] for o in range(PASSES)]]
-        key_scales = [
-            keep.tile([P, SLOTS], U8, name="key_scales0", align_bytes=64),
-            keep.tile([P, SLOTS], U8, name="key_scales1", align_bytes=64),
-        ]
+        pair_rows = keep.tile([P, 2, QUERIES, 2], BF16, name="pair_rows", align_bytes=64)
+        listed_scales = keep.tile([P, SLOTS], U8, name="listed_scales", align_bytes=64)
+        key_scales = keep.tile([P, PASSES, SLOTS], U8, name="key_scales", align_bytes=64)
         bias_row = keep.tile([P, SLOTS], F32, name="bias_row", align_bytes=64)
         bias_cols = reuse.tile([P, SLOTS // P], F32, name="bias_cols", align_bytes=64, offset=APART)
         bias_rows = late.tile([P, B, N], F32, name="bias_rows", align_bytes=64, offset=SLOTS)
@@ -112,17 +108,17 @@ def tile_attend_lq_score_kernel(tc, qT, k_words, k_scales, kb, offq, offs, out):
                     lhsT=q_codes[o][:, q_cols].bitcast(FP8X4),
                     lhsT_scale=q_scales[o][:, q_cols],
                     rhs=key_words[b][o][:, 2 * (g * P - b * N) : 2 * ((g + 1) * P - b * N)].bitcast(FP4X4),
-                    rhs_scale=key_scales[o][:, g * P : (g + 1) * P],
+                    rhs_scale=key_scales[:, o, g * P : (g + 1) * P],
                     start=(o == 0),
                     stop=(o == PASSES - 1),
                 )
 
         nc.scalar.activation(pair_pool[:], plane_pair[:].rearrange("p e c -> p c e"), COPY)
         nc.vector.tensor_copy(bias_row[:], bias_pool[:].indirect(slot_list[:]))
-        nc.vector.tensor_copy(key_scales[0][:], scale_pool[:].bitcast(U8).indirect(slot_list[:]))
-        grouped_words = grouped[0][:].rearrange("p q t -> p (q t)").bitcast(U32).rearrange("p (q u) -> p u q", u=2)
+        nc.vector.tensor_copy(listed_scales[:], scale_pool[:].bitcast(U8).indirect(slot_list[:]))
+        pair_words = pair_rows[:].rearrange("p u q e -> p (u q e)").bitcast(U32).rearrange("p (u q) -> p u q", u=2)
         pair_window = pair_pool[:].rearrange("p c e -> p (c e)").bitcast(U32)
-        nc.vector.tensor_copy(grouped_words[:, 1, :], pair_window.indirect(query_list[:]))
+        nc.vector.tensor_copy(pair_words[:, 1, :], pair_window.indirect(query_list[:]))
         for b in range(B):
             entries = slot_list[:, b * N // 16 : (b + 1) * N // 16]
             nc.vector.tensor_copy(key_pairs[b][:], word_pool[:].bitcast(U32).indirect(entries))
@@ -138,11 +134,16 @@ def tile_attend_lq_score_kernel(tc, qT, k_words, k_scales, kb, offq, offs, out):
                 first = b * N + j * P
                 nc.tensor.transpose(turned[b][:, j, :], bias_row[:, first : first + P], identity[:])
             nc.scalar.copy(bias_cols[:, b * (N // P) : (b + 1) * (N // P)], turned[b][:, :, BIAS_ROW])
-        nc.scalar.activation(grouped[0][:, :, 0], narrow[0][:].indirect(query_list[:]), COPY)
+        nc.scalar.activation(pair_rows[:, 0, :, 0], narrow[0][:].indirect(query_list[:]), COPY)
         nc.scalar.activation(narrow[1][:], first_planes[1][:], COPY)
-        nc.scalar.activation(grouped[0][:, :, 1], narrow[1][:].indirect(query_list[:]), COPY)
-        for r in range(4):
-            nc.sync.dma_start(key_scales[1][r:P:32, :].bitcast(I32), key_scales[0][SHIFT + r : P : 32, :].bitcast(I32))
+        nc.scalar.activation(pair_rows[:, 0, :, 1], narrow[1][:].indirect(query_list[:]), COPY)
+        grouped_words = grouped[0][:].rearrange("p q t -> p (q t)").bitcast(U32).rearrange("p (q u) -> p q u", u=2)
+        nc.scalar.copy(grouped_words, pair_words.rearrange("p u q -> p q u"))
+        nc.sync.dma_start(key_scales[0:4, :, :].bitcast(I32), listed_scales[0:32:4, :].bitcast(I32))
+        for o in range(PASSES):
+            for first in range(32, P, 32):
+                source = listed_scales[first + 4 * o : first + 32 : 8, :]
+                nc.sync.dma_start(key_scales[first : first + 4, o, :].bitcast(I32), source.bitcast(I32))
 
         for t in range(2):
             nc.vector.tensor_copy(picked[:, t, :], planes[t][:].indirect(query_list[:]))

@@ -1,7 +1,6 @@
 from contextlib import ExitStack
 
 import concourse.mybir as mybir
-from concourse.masks import make_identity
 
 F32 = mybir.dt.float32
 BF16 = mybir.dt.bfloat16
@@ -13,6 +12,8 @@ FP8X4 = mybir.dt.float8_e4m3fn_x4
 FP4X4 = mybir.dt.float4_e2m1fn_x4
 ADD = mybir.AluOpType.add
 COPY = mybir.ActivationFunctionType.Copy
+ABS = mybir.ActivationFunctionType.Abs
+RELU = mybir.ActivationFunctionType.Relu
 
 B, N, T, D, NQ, POOL = 2, 512, 2048, 1024, 128, 1024
 P = 128
@@ -21,9 +22,9 @@ PASSES = D // (P * PACK)
 SLOTS = B * N
 QUERIES = B * NQ
 BIAS_ROW = P - 1
+SCALE_ROW = 96
 HALF = N // 2
 BANK = 2048
-APART = 24 * 1024
 
 FLOPS = 2 * B * NQ * N * D
 
@@ -32,62 +33,50 @@ def tile_attend_lq_score_kernel(tc, qT, k_words, k_scales, kb, offq, offs, out):
     nc = tc.nc
     with ExitStack() as ctx:
         keep = ctx.enter_context(tc.tile_pool(name="keep", bufs=1))
-        reuse = ctx.enter_context(tc.tile_pool(name="reuse", bufs=1))
-        late = ctx.enter_context(tc.tile_pool(name="late", bufs=1))
         psum = ctx.enter_context(tc.psum_pool(name="psum", bufs=1))
 
         slot_list = keep.tile([P, SLOTS // 16], U16, name="slot_list")
         query_list = keep.tile([P, QUERIES // 16], U16, name="query_list")
         scale_pool = keep.tile([P, T // 4], I32, name="scale_pool", align_bytes=64)
         bias_pool = keep.tile([P, T], F32, name="bias_pool", align_bytes=64)
-        word_pool = reuse.tile([P, T], I32, name="word_pool", align_bytes=1024, offset=2 * APART)
+        word_pool = keep.tile([P, T], I32, name="word_pool", align_bytes=1024)
         identity = keep.tile([P, P], F32, name="identity", align_bytes=64)
-        first_planes = [
-            reuse.tile([P, POOL], F32, name="first_plane0", align_bytes=1024, offset=APART),
-            reuse.tile([P, POOL], F32, name="first_plane1", align_bytes=1024, offset=3 * APART),
-        ]
-        plane_pair = reuse.tile([P, 2, POOL], F32, name="plane_pair", align_bytes=1024, offset=12 * 1024)
-        planes = [reuse.tile([P, POOL], F32, name="plane%d" % t, align_bytes=1024, offset=APART * (t + 4)) for t in range(PACK)]
+        column_less_row = keep.tile([P, P], F32, name="column_less_row", align_bytes=64)
+        reuse = ctx.enter_context(tc.tile_pool(name="reuse", bufs=1))
+        distance = reuse.tile([P, P], F32, name="distance", align_bytes=1024, offset=16 * POOL)
+        plane_pairs = [keep.tile([P, 2, POOL], F32, name="plane_pair%d" % u, align_bytes=1024) for u in range(2)]
+        planes = [reuse.tile([P, POOL], F32, name="plane%d" % t, align_bytes=1024, offset=4 * POOL * t) for t in range(PACK)]
         q_rows = qT.rearrange("(o p t) c -> o p t c", o=PASSES, t=PACK)
 
-        nc.vector.memset(scale_pool[:], 0)
-        nc.vector.memset(bias_pool[0:BIAS_ROW, :], 0.0)
-        nc.vector.memset(identity[:], 0.0)
-        make_identity(nc, identity[:], nomemset=True)
         nc.sync.dma_start(slot_list[:], offs)
-        nc.scalar.dma_start(bias_pool[BIAS_ROW:P, :], kb[0:1, :])
-        nc.sync.dma_start(plane_pair[:], q_rows[0, :, 2:4, :])
-        nc.sync.dma_start(scale_pool[0:P:4, :], k_scales.bitcast(I32).rearrange("o f w -> f o w"))
-        nc.sync.dma_start(query_list[:], offq)
-        nc.sync.dma_start(first_planes[0][:], q_rows[0, :, 0, :])
+        nc.sync.dma_start(bias_pool[BIAS_ROW:P, :], kb[0:1, :])
+        nc.sync.dma_start(scale_pool[SCALE_ROW:P, :], k_scales.bitcast(I32).rearrange("o f w -> f o w"))
         nc.sync.dma_start(word_pool[:], k_words[0].rearrange("p t b -> p (t b)").bitcast(I32))
-        nc.sync.dma_start(first_planes[1][:], q_rows[0, :, 1, :])
+        nc.sync.dma_start(query_list[:], offq)
+        for u in range(2):
+            nc.sync.dma_start(plane_pairs[u][:], q_rows[0, :, 2 * u : 2 * u + 2, :])
         for t in range(PACK):
             nc.sync.dma_start(planes[t][:], q_rows[1, :, t, :])
+        nc.vector.memset(scale_pool[0:SCALE_ROW, :], 0)
+        nc.vector.memset(bias_pool[0:BIAS_ROW, :], 0.0)
+        nc.gpsimd.iota(column_less_row[:], [[1, P]], base=0, channel_multiplier=-1, allow_small_or_imprecise_dtypes=True)
+        nc.scalar.activation(distance[:], column_less_row[:], ABS)
+        nc.scalar.activation(identity[:], distance[:], RELU, bias=1.0, scale=-1.0)
 
-        narrow = [
-            keep.tile([P, POOL], BF16, name="narrow0", align_bytes=64),
-            late.tile([P, POOL], BF16, name="narrow1", align_bytes=64, offset=0),
-        ]
-        pair_pool = keep.tile([P, POOL, 2], BF16, name="pair_pool", align_bytes=64)
-        picked = keep.tile([P, 2, QUERIES], F32, name="picked", align_bytes=64)
+        picked = keep.tile([P, PACK, QUERIES], F32, name="picked", align_bytes=64)
         grouped = [keep.tile([P, QUERIES, PACK], BF16, name="grouped%d" % o, align_bytes=64) for o in range(PASSES)]
-        q_codes = [keep.tile([P, QUERIES], U32, name="q_codes%d" % o, align_bytes=64) for o in range(PASSES)]
+        q_codes = [
+            reuse.tile([P, QUERIES], U32, name="q_codes0", align_bytes=1024, offset=4 * POOL),
+            keep.tile([P, QUERIES], U32, name="q_codes1", align_bytes=64),
+        ]
         q_scales = [keep.tile([P, QUERIES], U8, name="q_scales%d" % o, align_bytes=64) for o in range(PASSES)]
         key_pairs = [keep.tile([P, N], U32, name="key_pairs%d" % b, align_bytes=64) for b in range(B)]
-        first_words = keep.tile([P, PASSES, 2 * N], U8, name="first_words", align_bytes=64)
-        second_words = [
-            keep.tile([P, 2 * N], U8, name="second_words0", align_bytes=64),
-            reuse.tile([P, 2 * N], U8, name="second_words1", align_bytes=64, offset=APART * (PACK + 3)),
-        ]
-        key_words = [[first_words[:, o, :] for o in range(PASSES)], [second_words[o][:] for o in range(PASSES)]]
-        pair_rows = keep.tile([P, 2, QUERIES, 2], BF16, name="pair_rows", align_bytes=64)
+        key_words = [keep.tile([P, PASSES, 2 * N], U8, name="key_words%d" % b, align_bytes=64) for b in range(B)]
         listed_scales = keep.tile([P, SLOTS], U8, name="listed_scales", align_bytes=64)
         key_scales = keep.tile([P, PASSES, SLOTS], U8, name="key_scales", align_bytes=64)
-        bias_row = keep.tile([P, SLOTS], F32, name="bias_row", align_bytes=64)
-        bias_cols = reuse.tile([P, SLOTS // P], F32, name="bias_cols", align_bytes=64, offset=APART)
-        bias_rows = late.tile([P, B, N], F32, name="bias_rows", align_bytes=64, offset=SLOTS)
-        bias = [bias_rows[:, b, :] for b in range(B)]
+        bias_row = reuse.tile([P, SLOTS], F32, name="bias_row", align_bytes=1024, offset=16 * POOL)
+        bias_cols = keep.tile([P, SLOTS // P], F32, name="bias_cols", align_bytes=64)
+        bias = [keep.tile([P, N], F32, name="bias%d" % b, align_bytes=64) for b in range(B)]
         result = [keep.tile([P, N], F32, name="result%d" % b, align_bytes=64) for b in range(B)]
         turned = [psum.tile([P, N // P, P], F32, name="turned%d" % b, offset=BANK * (4 + b)) for b in range(B)]
         spread = [psum.tile([P, N], F32, name="spread%d" % b, offset=BANK * (6 + b)) for b in range(B)]
@@ -102,59 +91,51 @@ def tile_attend_lq_score_kernel(tc, qT, k_words, k_scales, kb, offq, offs, out):
 
         def multiply(o, b):
             q_cols = slice(b * NQ, (b + 1) * NQ)
-            for g in range(b * N // P, (b + 1) * N // P):
+            for j in range(N // P):
+                g = b * N // P + j
                 nc.tensor.matmul_mx(
                     out=scores[g][:],
                     lhsT=q_codes[o][:, q_cols].bitcast(FP8X4),
                     lhsT_scale=q_scales[o][:, q_cols],
-                    rhs=key_words[b][o][:, 2 * (g * P - b * N) : 2 * ((g + 1) * P - b * N)].bitcast(FP4X4),
+                    rhs=key_words[b][:, o, 2 * j * P : 2 * (j + 1) * P].bitcast(FP4X4),
                     rhs_scale=key_scales[:, o, g * P : (g + 1) * P],
                     start=(o == 0),
                     stop=(o == PASSES - 1),
                 )
 
-        nc.scalar.activation(pair_pool[:], plane_pair[:].rearrange("p e c -> p c e"), COPY)
-        nc.vector.tensor_copy(bias_row[:], bias_pool[:].indirect(slot_list[:]))
         nc.vector.tensor_copy(listed_scales[:], scale_pool[:].bitcast(U8).indirect(slot_list[:]))
-        pair_words = pair_rows[:].rearrange("p u q e -> p (u q e)").bitcast(U32).rearrange("p (u q) -> p u q", u=2)
-        pair_window = pair_pool[:].rearrange("p c e -> p (c e)").bitcast(U32)
-        nc.vector.tensor_copy(pair_words[:, 1, :], pair_window.indirect(query_list[:]))
+        nc.scalar.activation(bias_row[:], bias_pool[:].indirect(slot_list[:]), COPY)
+        for quadrant in range(4):
+            source = listed_scales[SCALE_ROW + 8 * quadrant : SCALE_ROW + 8 * (quadrant + 1), :]
+            nc.sync.dma_start(key_scales[32 * quadrant : 32 * quadrant + 4, :, :].bitcast(I32), source.bitcast(I32))
         for b in range(B):
             entries = slot_list[:, b * N // 16 : (b + 1) * N // 16]
             nc.vector.tensor_copy(key_pairs[b][:], word_pool[:].bitcast(U32).indirect(entries))
-        halves = [key_pairs[b][:].bitcast(U16).rearrange("p (i o) -> p o i", o=PASSES) for b in range(B)]
-        nc.vector.tensor_copy(
-            first_words[:].rearrange("p o w -> p (o w)").bitcast(U16).rearrange("p (o i) -> p o i", o=PASSES), halves[0]
-        )
-        nc.vector.tensor_copy(second_words[0][:].bitcast(U16), halves[1][:, 0, :])
+        for b in range(B):
+            nc.vector.tensor_copy(
+                key_words[b][:].rearrange("p o w -> p (o w)").bitcast(U16).rearrange("p (o i) -> p o i", o=PASSES),
+                key_pairs[b][:].bitcast(U16).rearrange("p (i o) -> p o i", o=PASSES),
+            )
 
-        nc.scalar.activation(narrow[0][:], first_planes[0][:], COPY)
         for b in range(B):
             for j in range(N // P):
                 first = b * N + j * P
                 nc.tensor.transpose(turned[b][:, j, :], bias_row[:, first : first + P], identity[:])
             nc.scalar.copy(bias_cols[:, b * (N // P) : (b + 1) * (N // P)], turned[b][:, :, BIAS_ROW])
-        nc.scalar.activation(pair_rows[:, 0, :, 0], narrow[0][:].indirect(query_list[:]), COPY)
-        nc.scalar.activation(narrow[1][:], first_planes[1][:], COPY)
-        nc.scalar.activation(pair_rows[:, 0, :, 1], narrow[1][:].indirect(query_list[:]), COPY)
-        grouped_words = grouped[0][:].rearrange("p q t -> p (q t)").bitcast(U32).rearrange("p (q u) -> p q u", u=2)
-        nc.scalar.copy(grouped_words, pair_words.rearrange("p u q -> p q u"))
-        nc.sync.dma_start(key_scales[0:4, :, :].bitcast(I32), listed_scales[0:32:4, :].bitcast(I32))
-        for o in range(PASSES):
-            for first in range(32, P, 32):
-                source = listed_scales[first + 4 * o : first + 32 : 8, :]
-                nc.sync.dma_start(key_scales[first : first + 4, o, :].bitcast(I32), source.bitcast(I32))
-
-        for t in range(2):
-            nc.vector.tensor_copy(picked[:, t, :], planes[t][:].indirect(query_list[:]))
-        nc.scalar.copy(grouped[1][:, :, 0:2], picked[:].rearrange("p t q -> p q t"))
         for b in range(B):
             for j in range(N // P):
                 col = b * (N // P) + j
                 nc.tensor.transpose(
                     spread[b][:, j * P : (j + 1) * P], bias_cols[:, col : col + 1].to_broadcast([P, P]), identity[:]
                 )
-            nc.scalar.copy(bias[b], spread[b][:])
+            nc.scalar.copy(bias[b][:], spread[b][:])
+
+        for t in range(PACK - 1):
+            nc.scalar.activation(picked[:, t, :], plane_pairs[t // 2][:, t % 2, :].indirect(query_list[:]), COPY)
+        nc.vector.tensor_copy(picked[:, 3, :], plane_pairs[1][:, 1, :].indirect(query_list[:]))
+        nc.scalar.copy(grouped[0][:], picked[:].rearrange("p t q -> p q t"))
+        for t in range(2):
+            nc.vector.tensor_copy(grouped[1][:, :, t], planes[t][:].indirect(query_list[:]))
         quantize(0, slice(0, QUERIES))
         for b in range(B):
             multiply(0, b)
@@ -165,7 +146,6 @@ def tile_attend_lq_score_kernel(tc, qT, k_words, k_scales, kb, offq, offs, out):
             nc.vector.tensor_copy(grouped[1][:, q_cols, 3], planes[3][:].indirect(entries))
         for b in range(B):
             quantize(1, slice(b * NQ, (b + 1) * NQ))
-        nc.vector.tensor_copy(second_words[1][:].bitcast(U16), halves[1][:, 1, :])
         for b in range(B):
             multiply(1, b)
         for b in range(B):

@@ -22,7 +22,6 @@ PASSES = D // (P * PACK)
 SLOTS = B * N
 QUERIES = B * NQ
 BIAS_ROW = P - 1
-SCALE_ROW = 96
 HALF = N // 2
 BANK = 2048
 
@@ -43,27 +42,28 @@ def tile_attend_lq_score_kernel(tc, qT, k_words, k_scales, kb, offq, offs, out):
         identity = keep.tile([P, P], F32, name="identity", align_bytes=64)
         column_less_row = keep.tile([P, P], F32, name="column_less_row", align_bytes=64)
         reuse = ctx.enter_context(tc.tile_pool(name="reuse", bufs=1))
-        distance = reuse.tile([P, P], F32, name="distance", align_bytes=1024, offset=16 * POOL)
-        plane_pairs = [keep.tile([P, 2, POOL], F32, name="plane_pair%d" % u, align_bytes=1024) for u in range(2)]
+        distance = reuse.tile([P, P], F32, name="distance", align_bytes=256, offset=20 * POOL - 2 * P)
+        first_plane = keep.tile([P, POOL], F32, name="first_plane", align_bytes=1024)
+        plane_triple = keep.tile([P, 3, POOL], F32, name="plane_triple", align_bytes=1024)
         planes = [reuse.tile([P, POOL], F32, name="plane%d" % t, align_bytes=1024, offset=4 * POOL * t) for t in range(PACK)]
         q_rows = qT.rearrange("(o p t) c -> o p t c", o=PASSES, t=PACK)
 
+        nc.vector.memset(scale_pool[:], 0)
+        nc.scalar.dma_start(bias_pool[BIAS_ROW:P, :], kb[0:1, :])
         nc.sync.dma_start(slot_list[:], offs)
-        nc.sync.dma_start(bias_pool[BIAS_ROW:P, :], kb[0:1, :])
-        nc.sync.dma_start(scale_pool[SCALE_ROW:P, :], k_scales.bitcast(I32).rearrange("o f w -> f o w"))
-        nc.sync.dma_start(word_pool[:], k_words[0].rearrange("p t b -> p (t b)").bitcast(I32))
         nc.sync.dma_start(query_list[:], offq)
-        for u in range(2):
-            nc.sync.dma_start(plane_pairs[u][:], q_rows[0, :, 2 * u : 2 * u + 2, :])
+        nc.sync.dma_start(first_plane[:], q_rows[0, :, 0, :])
+        nc.sync.dma_start(scale_pool[0:P:4, :], k_scales.bitcast(I32).rearrange("o f w -> f o w"))
+        nc.sync.dma_start(word_pool[:], k_words[0].rearrange("p t b -> p (t b)").bitcast(I32))
+        nc.sync.dma_start(plane_triple[:], q_rows[0, :, 1:PACK, :])
         for t in range(PACK):
             nc.sync.dma_start(planes[t][:], q_rows[1, :, t, :])
-        nc.vector.memset(scale_pool[0:SCALE_ROW, :], 0)
         nc.vector.memset(bias_pool[0:BIAS_ROW, :], 0.0)
         nc.gpsimd.iota(column_less_row[:], [[1, P]], base=0, channel_multiplier=-1, allow_small_or_imprecise_dtypes=True)
         nc.scalar.activation(distance[:], column_less_row[:], ABS)
         nc.scalar.activation(identity[:], distance[:], RELU, bias=1.0, scale=-1.0)
 
-        picked = keep.tile([P, PACK, QUERIES], F32, name="picked", align_bytes=64)
+        picked = reuse.tile([P, PACK, QUERIES], F32, name="picked", align_bytes=1024, offset=16 * POOL)
         grouped = [keep.tile([P, QUERIES, PACK], BF16, name="grouped%d" % o, align_bytes=64) for o in range(PASSES)]
         q_codes = [
             reuse.tile([P, QUERIES], U32, name="q_codes0", align_bytes=1024, offset=4 * POOL),
@@ -73,8 +73,8 @@ def tile_attend_lq_score_kernel(tc, qT, k_words, k_scales, kb, offq, offs, out):
         key_pairs = [keep.tile([P, N], U32, name="key_pairs%d" % b, align_bytes=64) for b in range(B)]
         key_words = [keep.tile([P, PASSES, 2 * N], U8, name="key_words%d" % b, align_bytes=64) for b in range(B)]
         listed_scales = keep.tile([P, SLOTS], U8, name="listed_scales", align_bytes=64)
-        key_scales = keep.tile([P, PASSES, SLOTS], U8, name="key_scales", align_bytes=64)
-        bias_row = reuse.tile([P, SLOTS], F32, name="bias_row", align_bytes=1024, offset=16 * POOL)
+        key_scales = [keep.tile([P, SLOTS], U8, name="key_scales%d" % o, align_bytes=64) for o in range(PASSES)]
+        bias_row = reuse.tile([P, SLOTS], F32, name="bias_row", align_bytes=1024, offset=20 * POOL)
         bias_cols = keep.tile([P, SLOTS // P], F32, name="bias_cols", align_bytes=64)
         bias = [keep.tile([P, N], F32, name="bias%d" % b, align_bytes=64) for b in range(B)]
         result = [keep.tile([P, N], F32, name="result%d" % b, align_bytes=64) for b in range(B)]
@@ -98,16 +98,17 @@ def tile_attend_lq_score_kernel(tc, qT, k_words, k_scales, kb, offq, offs, out):
                     lhsT=q_codes[o][:, q_cols].bitcast(FP8X4),
                     lhsT_scale=q_scales[o][:, q_cols],
                     rhs=key_words[b][:, o, 2 * j * P : 2 * (j + 1) * P].bitcast(FP4X4),
-                    rhs_scale=key_scales[:, o, g * P : (g + 1) * P],
+                    rhs_scale=key_scales[o][:, g * P : (g + 1) * P],
                     start=(o == 0),
                     stop=(o == PASSES - 1),
                 )
 
         nc.vector.tensor_copy(listed_scales[:], scale_pool[:].bitcast(U8).indirect(slot_list[:]))
         nc.scalar.activation(bias_row[:], bias_pool[:].indirect(slot_list[:]), COPY)
-        for quadrant in range(4):
-            source = listed_scales[SCALE_ROW + 8 * quadrant : SCALE_ROW + 8 * (quadrant + 1), :]
-            nc.sync.dma_start(key_scales[32 * quadrant : 32 * quadrant + 4, :, :].bitcast(I32), source.bitcast(I32))
+        nc.vector.tensor_copy(key_scales[0][:].bitcast(I32), listed_scales[:].bitcast(I32))
+        for o in range(PASSES):
+            for r in range(1 - o, 4):
+                nc.sync.dma_start(key_scales[o][r:P:32, :].bitcast(I32), listed_scales[8 * r + 4 * o : P : 32, :].bitcast(I32))
         for b in range(B):
             entries = slot_list[:, b * N // 16 : (b + 1) * N // 16]
             nc.vector.tensor_copy(key_pairs[b][:], word_pool[:].bitcast(U32).indirect(entries))
@@ -130,9 +131,10 @@ def tile_attend_lq_score_kernel(tc, qT, k_words, k_scales, kb, offq, offs, out):
                 )
             nc.scalar.copy(bias[b][:], spread[b][:])
 
-        for t in range(PACK - 1):
-            nc.scalar.activation(picked[:, t, :], plane_pairs[t // 2][:, t % 2, :].indirect(query_list[:]), COPY)
-        nc.vector.tensor_copy(picked[:, 3, :], plane_pairs[1][:, 1, :].indirect(query_list[:]))
+        nc.scalar.activation(picked[:, 0, :], first_plane[:].indirect(query_list[:]), COPY)
+        for t in range(1, PACK - 1):
+            nc.scalar.activation(picked[:, t, :], plane_triple[:, t - 1, :].indirect(query_list[:]), COPY)
+        nc.vector.tensor_copy(picked[:, 3, :], plane_triple[:, 2, :].indirect(query_list[:]))
         nc.scalar.copy(grouped[0][:], picked[:].rearrange("p t q -> p q t"))
         for t in range(2):
             nc.vector.tensor_copy(grouped[1][:, :, t], planes[t][:].indirect(query_list[:]))

@@ -21,9 +21,10 @@ PACK = 4
 PASSES = D // (P * PACK)
 SLOTS = B * N
 QUERIES = B * NQ
+GROUPS = N // P
 BIAS_ROW = P - 1
-HALF = N // 2
 BANK = 2048
+EARLY = 8
 
 FLOPS = 2 * B * NQ * N * D
 
@@ -32,20 +33,22 @@ def tile_attend_lq_score_kernel(tc, qT, k_words, k_scales, kb, offq, offs, out):
     nc = tc.nc
     with ExitStack() as ctx:
         keep = ctx.enter_context(tc.tile_pool(name="keep", bufs=1))
+        reuse = ctx.enter_context(tc.tile_pool(name="reuse", bufs=1))
         psum = ctx.enter_context(tc.psum_pool(name="psum", bufs=1))
 
         slot_list = keep.tile([P, SLOTS // 16], U16, name="slot_list")
         query_list = keep.tile([P, QUERIES // 16], U16, name="query_list")
-        scale_pool = keep.tile([P, T // 4], I32, name="scale_pool", align_bytes=64)
-        bias_pool = keep.tile([P, T], F32, name="bias_pool", align_bytes=64)
-        word_pool = keep.tile([P, T], I32, name="word_pool", align_bytes=1024)
+        scale_pool = keep.tile([P, T // 4], I32, name="scale_pool", align_bytes=256)
+        bias_pool = keep.tile([P, T], F32, name="bias_pool", align_bytes=256)
+        word_pool = keep.tile([P, T], I32, name="word_pool", align_bytes=256)
         identity = keep.tile([P, P], F32, name="identity", align_bytes=64)
         column_less_row = keep.tile([P, P], F32, name="column_less_row", align_bytes=64)
-        reuse = ctx.enter_context(tc.tile_pool(name="reuse", bufs=1))
-        distance = reuse.tile([P, P], F32, name="distance", align_bytes=256, offset=20 * POOL - 2 * P)
-        first_plane = keep.tile([P, POOL], F32, name="first_plane", align_bytes=1024)
-        plane_triple = keep.tile([P, 3, POOL], F32, name="plane_triple", align_bytes=1024)
-        planes = [reuse.tile([P, POOL], F32, name="plane%d" % t, align_bytes=1024, offset=4 * POOL * t) for t in range(PACK)]
+        first_plane = keep.tile([P, POOL], F32, name="first_plane", align_bytes=256)
+        plane_triple = reuse.tile([P, 3 * POOL], F32, name="plane_triple", align_bytes=256, offset=0)
+        plane_pair = keep.tile([P, 2 * POOL], F32, name="plane_pair", align_bytes=256)
+        third_plane = keep.tile([P, POOL], F32, name="third_plane", align_bytes=256)
+        last_plane = keep.tile([P, POOL], F32, name="last_plane", align_bytes=256)
+        distance = reuse.tile([P, P], F32, name="distance", align_bytes=256, offset=14 * POOL - 2 * P)
         q_rows = qT.rearrange("(o p t) c -> o p t c", o=PASSES, t=PACK)
 
         nc.vector.memset(scale_pool[:], 0)
@@ -55,32 +58,35 @@ def tile_attend_lq_score_kernel(tc, qT, k_words, k_scales, kb, offq, offs, out):
         nc.sync.dma_start(first_plane[:], q_rows[0, :, 0, :])
         nc.sync.dma_start(scale_pool[0:P:4, :], k_scales.bitcast(I32).rearrange("o f w -> f o w"))
         nc.sync.dma_start(word_pool[:], k_words[0].rearrange("p t b -> p (t b)").bitcast(I32))
-        nc.sync.dma_start(plane_triple[:], q_rows[0, :, 1:PACK, :])
-        for t in range(PACK):
-            nc.sync.dma_start(planes[t][:], q_rows[1, :, t, :])
+        nc.sync.dma_start(plane_triple[:], q_rows[0, :, 1:PACK, :].rearrange("p t c -> p (t c)"))
+        nc.sync.dma_start(plane_pair[:], q_rows[1, :, 1:3, :].rearrange("p t c -> p (t c)"))
+        nc.sync.dma_start(third_plane[:], q_rows[1, :, 3, :])
+        nc.sync.dma_start(last_plane[:], q_rows[1, :, 0, :])
         nc.vector.memset(bias_pool[0:BIAS_ROW, :], 0.0)
         nc.gpsimd.iota(column_less_row[:], [[1, P]], base=0, channel_multiplier=-1, allow_small_or_imprecise_dtypes=True)
         nc.scalar.activation(distance[:], column_less_row[:], ABS)
         nc.scalar.activation(identity[:], distance[:], RELU, bias=1.0, scale=-1.0)
 
-        picked = reuse.tile([P, PACK, QUERIES], F32, name="picked", align_bytes=1024, offset=16 * POOL)
-        grouped = [keep.tile([P, QUERIES, PACK], BF16, name="grouped%d" % o, align_bytes=64) for o in range(PASSES)]
-        q_codes = [
-            reuse.tile([P, QUERIES], U32, name="q_codes0", align_bytes=1024, offset=4 * POOL),
-            keep.tile([P, QUERIES], U32, name="q_codes1", align_bytes=64),
+        grouped = [
+            reuse.tile([P, QUERIES, PACK], BF16, name="grouped0", align_bytes=256, offset=12 * POOL),
+            reuse.tile([P, QUERIES, PACK], BF16, name="grouped1", align_bytes=256, offset=0),
         ]
+        bias_row = reuse.tile([P, SLOTS], F32, name="bias_row", align_bytes=256, offset=14 * POOL)
+        q_codes = [keep.tile([P, QUERIES], U32, name="q_codes%d" % o, align_bytes=64) for o in range(PASSES)]
         q_scales = [keep.tile([P, QUERIES], U8, name="q_scales%d" % o, align_bytes=64) for o in range(PASSES)]
         key_pairs = [keep.tile([P, N], U32, name="key_pairs%d" % b, align_bytes=64) for b in range(B)]
         key_words = [keep.tile([P, PASSES, 2 * N], U8, name="key_words%d" % b, align_bytes=64) for b in range(B)]
         listed_scales = keep.tile([P, SLOTS], U8, name="listed_scales", align_bytes=64)
-        key_scales = [keep.tile([P, SLOTS], U8, name="key_scales%d" % o, align_bytes=64) for o in range(PASSES)]
-        bias_row = reuse.tile([P, SLOTS], F32, name="bias_row", align_bytes=1024, offset=20 * POOL)
+        key_scales = keep.tile([P, B * PASSES * N], U8, name="key_scales", align_bytes=64)
         bias_cols = keep.tile([P, SLOTS // P], F32, name="bias_cols", align_bytes=64)
         bias = [keep.tile([P, N], F32, name="bias%d" % b, align_bytes=64) for b in range(B)]
         result = [keep.tile([P, N], F32, name="result%d" % b, align_bytes=64) for b in range(B)]
-        turned = [psum.tile([P, N // P, P], F32, name="turned%d" % b, offset=BANK * (4 + b)) for b in range(B)]
+        turned = [psum.tile([P, GROUPS, P], F32, name="turned%d" % b, offset=BANK * (4 + b)) for b in range(B)]
         spread = [psum.tile([P, N], F32, name="spread%d" % b, offset=BANK * (6 + b)) for b in range(B)]
-        scores = [psum.tile([P, P], F32, name="scores%d" % g, offset=BANK * g) for g in range(SLOTS // P)]
+        scores = [
+            [psum.tile([P, P], F32, name="scores%d_%d" % (b, j), offset=BANK * ((b * GROUPS + j) % EARLY)) for j in range(GROUPS)]
+            for b in range(B)
+        ]
 
         def quantize(o, cols):
             nc.vector.quantize_mx(
@@ -89,26 +95,35 @@ def tile_attend_lq_score_kernel(tc, qT, k_words, k_scales, kb, offq, offs, out):
                 in_=grouped[o][:, cols, :].rearrange("p q t -> p (q t)"),
             )
 
-        def multiply(o, b):
+        def multiply(o, b, j):
             q_cols = slice(b * NQ, (b + 1) * NQ)
-            for j in range(N // P):
-                g = b * N // P + j
-                nc.tensor.matmul_mx(
-                    out=scores[g][:],
-                    lhsT=q_codes[o][:, q_cols].bitcast(FP8X4),
-                    lhsT_scale=q_scales[o][:, q_cols],
-                    rhs=key_words[b][:, o, 2 * j * P : 2 * (j + 1) * P].bitcast(FP4X4),
-                    rhs_scale=key_scales[o][:, g * P : (g + 1) * P],
-                    start=(o == 0),
-                    stop=(o == PASSES - 1),
-                )
+            first = o * SLOTS + b * N + j * P
+            nc.tensor.matmul_mx(
+                out=scores[b][j][:],
+                lhsT=q_codes[o][:, q_cols].bitcast(FP8X4),
+                lhsT_scale=q_scales[o][:, q_cols],
+                rhs=key_words[b][:, o, 2 * j * P : 2 * (j + 1) * P].bitcast(FP4X4),
+                rhs_scale=key_scales[:, first : first + P],
+                start=(o == 0),
+                stop=(o == PASSES - 1),
+            )
+
+        def add_bias(b, j):
+            part = slice(j * P, (j + 1) * P)
+            nc.vector.tensor_tensor(result[b][:, part], scores[b][j][:], bias[b][:, part], ADD)
+
+        def store(b, first, last):
+            cols = slice(first * P, last * P)
+            nc.sync.dma_start(out[b, :, cols], result[b][:, cols])
 
         nc.vector.tensor_copy(listed_scales[:], scale_pool[:].bitcast(U8).indirect(slot_list[:]))
         nc.scalar.activation(bias_row[:], bias_pool[:].indirect(slot_list[:]), COPY)
-        nc.vector.tensor_copy(key_scales[0][:].bitcast(I32), listed_scales[:].bitcast(I32))
+        listed = listed_scales[:].bitcast(I32)
+        placed = key_scales[:].bitcast(I32).rearrange("p (o w) -> p o w", o=PASSES)
+        nc.vector.tensor_copy(placed[:, 0, :], listed)
         for o in range(PASSES):
             for r in range(1 - o, 4):
-                nc.sync.dma_start(key_scales[o][r:P:32, :].bitcast(I32), listed_scales[8 * r + 4 * o : P : 32, :].bitcast(I32))
+                nc.sync.dma_start(placed[r:P:32, o, :], listed[8 * r + 4 * o : P : 32, :])
         for b in range(B):
             entries = slot_list[:, b * N // 16 : (b + 1) * N // 16]
             nc.vector.tensor_copy(key_pairs[b][:], word_pool[:].bitcast(U32).indirect(entries))
@@ -119,42 +134,40 @@ def tile_attend_lq_score_kernel(tc, qT, k_words, k_scales, kb, offq, offs, out):
             )
 
         for b in range(B):
-            for j in range(N // P):
+            for j in range(GROUPS):
                 first = b * N + j * P
                 nc.tensor.transpose(turned[b][:, j, :], bias_row[:, first : first + P], identity[:])
-            nc.scalar.copy(bias_cols[:, b * (N // P) : (b + 1) * (N // P)], turned[b][:, :, BIAS_ROW])
+            nc.scalar.copy(bias_cols[:, b * GROUPS : (b + 1) * GROUPS], turned[b][:, :, BIAS_ROW])
         for b in range(B):
-            for j in range(N // P):
-                col = b * (N // P) + j
+            for j in range(GROUPS):
+                col = b * GROUPS + j
                 nc.tensor.transpose(
                     spread[b][:, j * P : (j + 1) * P], bias_cols[:, col : col + 1].to_broadcast([P, P]), identity[:]
                 )
             nc.scalar.copy(bias[b][:], spread[b][:])
 
-        nc.scalar.activation(picked[:, 0, :], first_plane[:].indirect(query_list[:]), COPY)
-        for t in range(1, PACK - 1):
-            nc.scalar.activation(picked[:, t, :], plane_triple[:, t - 1, :].indirect(query_list[:]), COPY)
-        nc.vector.tensor_copy(picked[:, 3, :], plane_triple[:, 2, :].indirect(query_list[:]))
-        nc.scalar.copy(grouped[0][:], picked[:].rearrange("p t q -> p q t"))
-        for t in range(2):
-            nc.vector.tensor_copy(grouped[1][:, :, t], planes[t][:].indirect(query_list[:]))
+        nc.scalar.activation(grouped[0][:, :, 0], first_plane[:].indirect(query_list[:]), COPY)
+        nc.scalar.activation(grouped[0][:, :, 1], plane_triple[:].indirect(query_list[:]), COPY)
+        for t in range(2, PACK):
+            nc.vector.tensor_copy(grouped[0][:, :, t], plane_triple[:, (t - 1) * POOL : t * POOL].indirect(query_list[:]))
         quantize(0, slice(0, QUERIES))
-        for b in range(B):
-            multiply(0, b)
-        nc.vector.tensor_copy(grouped[1][:, :, 2], planes[2][:].indirect(query_list[:]))
+        nc.scalar.activation(grouped[1][:, :, 1], plane_pair[:].indirect(query_list[:]), COPY)
+        nc.vector.tensor_copy(grouped[1][:, :, 2], plane_pair[:, POOL : 2 * POOL].indirect(query_list[:]))
+        nc.vector.tensor_copy(grouped[1][:, :, 3], third_plane[:].indirect(query_list[:]))
         for b in range(B):
             q_cols = slice(b * NQ, (b + 1) * NQ)
             entries = query_list[:, b * NQ // 16 : (b + 1) * NQ // 16]
-            nc.vector.tensor_copy(grouped[1][:, q_cols, 3], planes[3][:].indirect(entries))
+            nc.scalar.activation(grouped[1][:, q_cols, 0], last_plane[:].indirect(entries), COPY)
         for b in range(B):
             quantize(1, slice(b * NQ, (b + 1) * NQ))
-        for b in range(B):
-            multiply(1, b)
-        for b in range(B):
-            for h in range(2):
-                cols = slice(h * HALF, (h + 1) * HALF)
-                for j in range(2 * h, 2 * h + 2):
-                    part = slice(j * P, (j + 1) * P)
-                    nc.vector.tensor_tensor(result[b][:, part], scores[b * N // P + j][:], bias[b][:, part], ADD)
-                queue = nc.sync if h == 0 else nc.scalar
-                queue.dma_start(out[b, :, cols], result[b][:, cols])
+
+        for g in range(EARLY):
+            multiply(0, g // GROUPS, g % GROUPS)
+        for g in range(B * GROUPS):
+            b, j = divmod(g, GROUPS)
+            if g >= EARLY:
+                multiply(0, b, j)
+            multiply(1, b, j)
+            add_bias(b, j)
+            if j % 2 == 1:
+                store(b, j - 1, j + 1)

@@ -45,8 +45,7 @@ def tile_attend_lq_score_kernel(tc, qT, k_words, k_scales, kb, offq, offs, out):
         column_less_row = keep.tile([P, P], F32, name="column_less_row", align_bytes=64)
         first_plane = keep.tile([P, POOL], F32, name="first_plane", align_bytes=256)
         plane_triple = reuse.tile([P, 3 * POOL], F32, name="plane_triple", align_bytes=256, offset=0)
-        plane_pair = keep.tile([P, 2 * POOL], F32, name="plane_pair", align_bytes=256)
-        third_plane = keep.tile([P, POOL], F32, name="third_plane", align_bytes=256)
+        late_triple = keep.tile([P, 3 * POOL], F32, name="late_triple", align_bytes=256)
         last_plane = keep.tile([P, POOL], F32, name="last_plane", align_bytes=256)
         distance = reuse.tile([P, P], F32, name="distance", align_bytes=256, offset=14 * POOL - 2 * P)
         q_rows = qT.rearrange("(o p t) c -> o p t c", o=PASSES, t=PACK)
@@ -59,8 +58,7 @@ def tile_attend_lq_score_kernel(tc, qT, k_words, k_scales, kb, offq, offs, out):
         nc.sync.dma_start(scale_pool[0:P:4, :], k_scales.bitcast(I32).rearrange("o f w -> f o w"))
         nc.sync.dma_start(word_pool[:], k_words[0].rearrange("p t b -> p (t b)").bitcast(I32))
         nc.sync.dma_start(plane_triple[:], q_rows[0, :, 1:PACK, :].rearrange("p t c -> p (t c)"))
-        nc.sync.dma_start(plane_pair[:], q_rows[1, :, 1:3, :].rearrange("p t c -> p (t c)"))
-        nc.sync.dma_start(third_plane[:], q_rows[1, :, 3, :])
+        nc.sync.dma_start(late_triple[:], q_rows[1, :, 1:PACK, :].rearrange("p t c -> p (t c)"))
         nc.sync.dma_start(last_plane[:], q_rows[1, :, 0, :])
         nc.vector.memset(bias_pool[0:BIAS_ROW, :], 0.0)
         nc.gpsimd.iota(column_less_row[:], [[1, P]], base=0, channel_multiplier=-1, allow_small_or_imprecise_dtypes=True)
@@ -151,13 +149,16 @@ def tile_attend_lq_score_kernel(tc, qT, k_words, k_scales, kb, offq, offs, out):
         for t in range(2, PACK):
             nc.vector.tensor_copy(grouped[0][:, :, t], plane_triple[:, (t - 1) * POOL : t * POOL].indirect(query_list[:]))
         quantize(0, slice(0, QUERIES))
-        nc.scalar.activation(grouped[1][:, :, 1], plane_pair[:].indirect(query_list[:]), COPY)
-        nc.vector.tensor_copy(grouped[1][:, :, 2], plane_pair[:, POOL : 2 * POOL].indirect(query_list[:]))
-        nc.vector.tensor_copy(grouped[1][:, :, 3], third_plane[:].indirect(query_list[:]))
+        for window, t in ((late_triple, 1), (last_plane, 0)):
+            for b in range(B):
+                q_cols = slice(b * NQ, (b + 1) * NQ)
+                entries = query_list[:, b * NQ // 16 : (b + 1) * NQ // 16]
+                nc.scalar.activation(grouped[1][:, q_cols, t], window[:].indirect(entries), COPY)
         for b in range(B):
             q_cols = slice(b * NQ, (b + 1) * NQ)
             entries = query_list[:, b * NQ // 16 : (b + 1) * NQ // 16]
-            nc.scalar.activation(grouped[1][:, q_cols, 0], last_plane[:].indirect(entries), COPY)
+            for t in range(2, PACK):
+                nc.vector.tensor_copy(grouped[1][:, q_cols, t], late_triple[:, (t - 1) * POOL : t * POOL].indirect(entries))
         for b in range(B):
             quantize(1, slice(b * NQ, (b + 1) * NQ))
 

@@ -25,6 +25,7 @@ GROUPS = N // P
 BIAS_ROW = P - 1
 BANK = 2048
 EARLY = 8
+SOON = 7 * P // 4
 
 FLOPS = 2 * B * NQ * N * D
 
@@ -70,6 +71,7 @@ def tile_attend_lq_score_kernel(tc, qT, k_words, k_scales, kb, offq, offs, out):
             reuse.tile([P, QUERIES, PACK], BF16, name="grouped1", align_bytes=256, offset=0),
         ]
         bias_row = reuse.tile([P, SLOTS], F32, name="bias_row", align_bytes=256, offset=14 * POOL)
+        picked = reuse.tile([P, B, 2, NQ], F32, name="picked", align_bytes=256, offset=2 * POOL)
         q_codes = [keep.tile([P, QUERIES], U32, name="q_codes%d" % o, align_bytes=64) for o in range(PASSES)]
         q_scales = [keep.tile([P, QUERIES], U8, name="q_scales%d" % o, align_bytes=64) for o in range(PASSES)]
         key_pairs = [keep.tile([P, N], U32, name="key_pairs%d" % b, align_bytes=64) for b in range(B)]
@@ -119,9 +121,11 @@ def tile_attend_lq_score_kernel(tc, qT, k_words, k_scales, kb, offq, offs, out):
         listed = listed_scales[:].bitcast(I32)
         placed = key_scales[:].bitcast(I32).rearrange("p (o w) -> p o w", o=PASSES)
         nc.vector.tensor_copy(placed[:, 0, :], listed)
-        for o in range(PASSES):
-            for r in range(1 - o, 4):
-                nc.sync.dma_start(placed[r:P:32, o, :], listed[8 * r + 4 * o : P : 32, :])
+        for r in range(1, 4):
+            nc.sync.dma_start(placed[r:P:32, 0, :], listed[8 * r : P : 32, :])
+        for words in (slice(0, SOON), slice(SOON, SLOTS // 4)):
+            for r in range(4):
+                nc.sync.dma_start(placed[r:P:32, 1, words], listed[8 * r + 4 : P : 32, words])
         for b in range(B):
             entries = slot_list[:, b * N // 16 : (b + 1) * N // 16]
             nc.vector.tensor_copy(key_pairs[b][:], word_pool[:].bitcast(U32).indirect(entries))
@@ -158,7 +162,9 @@ def tile_attend_lq_score_kernel(tc, qT, k_words, k_scales, kb, offq, offs, out):
             q_cols = slice(b * NQ, (b + 1) * NQ)
             entries = query_list[:, b * NQ // 16 : (b + 1) * NQ // 16]
             for t in range(2, PACK):
-                nc.vector.tensor_copy(grouped[1][:, q_cols, t], late_triple[:, (t - 1) * POOL : t * POOL].indirect(entries))
+                nc.vector.tensor_copy(picked[:, b, t - 2, :], late_triple[:, (t - 1) * POOL : t * POOL].indirect(entries))
+        for b in range(B):
+            nc.vector.tensor_copy(grouped[1][:, b * NQ : (b + 1) * NQ, 2:PACK], picked[:, b, :, :].rearrange("p t q -> p q t"))
         for b in range(B):
             quantize(1, slice(b * NQ, (b + 1) * NQ))
 

@@ -71,7 +71,7 @@ def tile_attend_lq_score_kernel(tc, qT, k_words, k_scales, kb, offq, offs, out):
             reuse.tile([P, QUERIES, PACK], BF16, name="grouped1", align_bytes=256, offset=0),
         ]
         bias_row = reuse.tile([P, SLOTS], F32, name="bias_row", align_bytes=256, offset=14 * POOL)
-        picked = reuse.tile([P, B, 2, NQ], F32, name="picked", align_bytes=256, offset=2 * POOL)
+        picked = reuse.tile([P, B, 2, NQ], F32, name="picked", align_bytes=256, offset=12 * POOL)
         q_codes = [keep.tile([P, QUERIES], U32, name="q_codes%d" % o, align_bytes=64) for o in range(PASSES)]
         q_scales = [keep.tile([P, QUERIES], U8, name="q_scales%d" % o, align_bytes=64) for o in range(PASSES)]
         key_pairs = [keep.tile([P, N], U32, name="key_pairs%d" % b, align_bytes=64) for b in range(B)]
@@ -123,8 +123,9 @@ def tile_attend_lq_score_kernel(tc, qT, k_words, k_scales, kb, offq, offs, out):
         nc.vector.tensor_copy(placed[:, 0, :], listed)
         for r in range(1, 4):
             nc.sync.dma_start(placed[r:P:32, 0, :], listed[8 * r : P : 32, :])
+        nc.sync.dma_start(placed[0:P:32, 1, :], listed[4:P:32, :])
         for words in (slice(0, SOON), slice(SOON, SLOTS // 4)):
-            for r in range(4):
+            for r in range(1, 4):
                 nc.sync.dma_start(placed[r:P:32, 1, words], listed[8 * r + 4 : P : 32, words])
         for b in range(B):
             entries = slot_list[:, b * N // 16 : (b + 1) * N // 16]
@@ -153,11 +154,11 @@ def tile_attend_lq_score_kernel(tc, qT, k_words, k_scales, kb, offq, offs, out):
         for t in range(2, PACK):
             nc.vector.tensor_copy(grouped[0][:, :, t], plane_triple[:, (t - 1) * POOL : t * POOL].indirect(query_list[:]))
         quantize(0, slice(0, QUERIES))
-        for window, t in ((late_triple, 1), (last_plane, 0)):
-            for b in range(B):
-                q_cols = slice(b * NQ, (b + 1) * NQ)
-                entries = query_list[:, b * NQ // 16 : (b + 1) * NQ // 16]
-                nc.scalar.activation(grouped[1][:, q_cols, t], window[:].indirect(entries), COPY)
+        nc.scalar.activation(grouped[1][:, :, 1], late_triple[:].indirect(query_list[:]), COPY)
+        pieces = [slice(0, NQ // 2), slice(NQ // 2, NQ), slice(NQ, QUERIES)]
+        for cols in pieces:
+            entries = query_list[:, cols.start // 16 : cols.stop // 16]
+            nc.scalar.activation(grouped[1][:, cols, 0], last_plane[:].indirect(entries), COPY)
         for b in range(B):
             q_cols = slice(b * NQ, (b + 1) * NQ)
             entries = query_list[:, b * NQ // 16 : (b + 1) * NQ // 16]
@@ -165,8 +166,8 @@ def tile_attend_lq_score_kernel(tc, qT, k_words, k_scales, kb, offq, offs, out):
                 nc.vector.tensor_copy(picked[:, b, t - 2, :], late_triple[:, (t - 1) * POOL : t * POOL].indirect(entries))
         for b in range(B):
             nc.vector.tensor_copy(grouped[1][:, b * NQ : (b + 1) * NQ, 2:PACK], picked[:, b, :, :].rearrange("p t q -> p q t"))
-        for b in range(B):
-            quantize(1, slice(b * NQ, (b + 1) * NQ))
+        for cols in pieces:
+            quantize(1, cols)
 
         for g in range(EARLY):
             multiply(0, g // GROUPS, g % GROUPS)
@@ -176,5 +177,7 @@ def tile_attend_lq_score_kernel(tc, qT, k_words, k_scales, kb, offq, offs, out):
                 multiply(0, b, j)
             multiply(1, b, j)
             add_bias(b, j)
-            if j % 2 == 1:
+            if g < 2:
+                store(b, j, j + 1)
+            elif j % 2 == 1:
                 store(b, j - 1, j + 1)

from contextlib import ExitStack

import concourse.mybir as mybir

F32 = mybir.dt.float32
BF16 = mybir.dt.bfloat16
I32 = mybir.dt.int32
U32 = mybir.dt.uint32
U16 = mybir.dt.uint16
U8 = mybir.dt.uint8
FP8X4 = mybir.dt.float8_e4m3fn_x4
FP4X4 = mybir.dt.float4_e2m1fn_x4
ADD = mybir.AluOpType.add
COPY = mybir.ActivationFunctionType.Copy
ABS = mybir.ActivationFunctionType.Abs
RELU = mybir.ActivationFunctionType.Relu

B, N, T, D, NQ, POOL = 2, 512, 2048, 1024, 128, 1024
P = 128
PACK = 4
PASSES = D // (P * PACK)
SLOTS = B * N
QUERIES = B * NQ
GROUPS = N // P
BIAS_ROW = P - 1
BANK = 2048
EARLY = 8
SOON = 7 * P // 4

FLOPS = 2 * B * NQ * N * D


def tile_attend_lq_score_kernel(tc, qT, k_words, k_scales, kb, offq, offs, out):
    nc = tc.nc
    with ExitStack() as ctx:
        keep = ctx.enter_context(tc.tile_pool(name="keep", bufs=1))
        reuse = ctx.enter_context(tc.tile_pool(name="reuse", bufs=1))
        psum = ctx.enter_context(tc.psum_pool(name="psum", bufs=1))

        slot_list = keep.tile([P, SLOTS // 16], U16, name="slot_list")
        query_list = keep.tile([P, QUERIES // 16], U16, name="query_list")
        scale_pool = keep.tile([P, T // 4], I32, name="scale_pool", align_bytes=256)
        bias_pool = keep.tile([P, T], F32, name="bias_pool", align_bytes=256)
        word_pool = keep.tile([P, T], I32, name="word_pool", align_bytes=256)
        identity = keep.tile([P, P], F32, name="identity", align_bytes=64)
        column_less_row = keep.tile([P, P], F32, name="column_less_row", align_bytes=64)
        first_plane = keep.tile([P, POOL], F32, name="first_plane", align_bytes=256)
        plane_triple = reuse.tile([P, 3 * POOL], F32, name="plane_triple", align_bytes=256, offset=0)
        late_triple = keep.tile([P, 3 * POOL], F32, name="late_triple", align_bytes=256)
        last_plane = keep.tile([P, POOL], F32, name="last_plane", align_bytes=256)
        distance = reuse.tile([P, P], F32, name="distance", align_bytes=256, offset=14 * POOL - 2 * P)
        q_rows = qT.rearrange("(o p t) c -> o p t c", o=PASSES, t=PACK)

        nc.vector.memset(scale_pool[:], 0)
        nc.scalar.dma_start(bias_pool[BIAS_ROW:P, :], kb[0:1, :])
        nc.sync.dma_start(slot_list[:], offs)
        nc.sync.dma_start(query_list[:], offq)
        nc.sync.dma_start(first_plane[:], q_rows[0, :, 0, :])
        nc.sync.dma_start(scale_pool[0:P:4, :], k_scales.bitcast(I32).rearrange("o f w -> f o w"))
        nc.sync.dma_start(word_pool[:], k_words[0].rearrange("p t b -> p (t b)").bitcast(I32))
        nc.sync.dma_start(plane_triple[:], q_rows[0, :, 1:PACK, :].rearrange("p t c -> p (t c)"))
        nc.sync.dma_start(late_triple[:], q_rows[1, :, 1:PACK, :].rearrange("p t c -> p (t c)"))
        nc.sync.dma_start(last_plane[:], q_rows[1, :, 0, :])
        nc.vector.memset(bias_pool[0:BIAS_ROW, :], 0.0)
        nc.gpsimd.iota(column_less_row[:], [[1, P]], base=0, channel_multiplier=-1, allow_small_or_imprecise_dtypes=True)
        nc.scalar.activation(distance[:], column_less_row[:], ABS)
        nc.scalar.activation(identity[:], distance[:], RELU, bias=1.0, scale=-1.0)

        grouped = [
            reuse.tile([P, QUERIES, PACK], BF16, name="grouped0", align_bytes=256, offset=12 * POOL),
            reuse.tile([P, QUERIES, PACK], BF16, name="grouped1", align_bytes=256, offset=0),
        ]
        bias_row = reuse.tile([P, SLOTS], F32, name="bias_row", align_bytes=256, offset=14 * POOL)
        picked = reuse.tile([P, B, 2, NQ], F32, name="picked", align_bytes=256, offset=12 * POOL)
        q_codes = [keep.tile([P, QUERIES], U32, name="q_codes%d" % o, align_bytes=64) for o in range(PASSES)]
        q_scales = [keep.tile([P, QUERIES], U8, name="q_scales%d" % o, align_bytes=64) for o in range(PASSES)]
        key_pairs = [keep.tile([P, N], U32, name="key_pairs%d" % b, align_bytes=64) for b in range(B)]
        key_words = [keep.tile([P, PASSES, 2 * N], U8, name="key_words%d" % b, align_bytes=64) for b in range(B)]
        listed_scales = keep.tile([P, SLOTS], U8, name="listed_scales", align_bytes=64)
        key_scales = keep.tile([P, B * PASSES * N], U8, name="key_scales", align_bytes=64)
        bias_cols = keep.tile([P, SLOTS // P], F32, name="bias_cols", align_bytes=64)
        bias = [keep.tile([P, N], F32, name="bias%d" % b, align_bytes=64) for b in range(B)]
        result = [keep.tile([P, N], F32, name="result%d" % b, align_bytes=64) for b in range(B)]
        turned = [psum.tile([P, GROUPS, P], F32, name="turned%d" % b, offset=BANK * (4 + b)) for b in range(B)]
        spread = [psum.tile([P, N], F32, name="spread%d" % b, offset=BANK * (6 + b)) for b in range(B)]
        scores = [
            [psum.tile([P, P], F32, name="scores%d_%d" % (b, j), offset=BANK * ((b * GROUPS + j) % EARLY)) for j in range(GROUPS)]
            for b in range(B)
        ]

        def quantize(o, cols):
            nc.vector.quantize_mx(
                out=q_codes[o][:, cols].bitcast(FP8X4),
                scales=q_scales[o][:, cols],
                in_=grouped[o][:, cols, :].rearrange("p q t -> p (q t)"),
            )

        def multiply(o, b, j):
            q_cols = slice(b * NQ, (b + 1) * NQ)
            first = o * SLOTS + b * N + j * P
            nc.tensor.matmul_mx(
                out=scores[b][j][:],
                lhsT=q_codes[o][:, q_cols].bitcast(FP8X4),
                lhsT_scale=q_scales[o][:, q_cols],
                rhs=key_words[b][:, o, 2 * j * P : 2 * (j + 1) * P].bitcast(FP4X4),
                rhs_scale=key_scales[:, first : first + P],
                start=(o == 0),
                stop=(o == PASSES - 1),
            )

        def add_bias(b, j):
            part = slice(j * P, (j + 1) * P)
            nc.vector.tensor_tensor(result[b][:, part], scores[b][j][:], bias[b][:, part], ADD)

        def store(b, first, last):
            cols = slice(first * P, last * P)
            nc.sync.dma_start(out[b, :, cols], result[b][:, cols])

        nc.vector.tensor_copy(listed_scales[:], scale_pool[:].bitcast(U8).indirect(slot_list[:]))
        nc.scalar.activation(bias_row[:], bias_pool[:].indirect(slot_list[:]), COPY)
        listed = listed_scales[:].bitcast(I32)
        placed = key_scales[:].bitcast(I32).rearrange("p (o w) -> p o w", o=PASSES)
        nc.vector.tensor_copy(placed[:, 0, :], listed)
        for r in range(1, 4):
            nc.sync.dma_start(placed[r:P:32, 0, :], listed[8 * r : P : 32, :])
        nc.sync.dma_start(placed[0:P:32, 1, :], listed[4:P:32, :])
        for words in (slice(0, SOON), slice(SOON, SLOTS // 4)):
            for r in range(1, 4):
                nc.sync.dma_start(placed[r:P:32, 1, words], listed[8 * r + 4 : P : 32, words])
        for b in range(B):
            entries = slot_list[:, b * N // 16 : (b + 1) * N // 16]
            nc.vector.tensor_copy(key_pairs[b][:], word_pool[:].bitcast(U32).indirect(entries))
        for b in range(B):
            nc.vector.tensor_copy(
                key_words[b][:].rearrange("p o w -> p (o w)").bitcast(U16).rearrange("p (o i) -> p o i", o=PASSES),
                key_pairs[b][:].bitcast(U16).rearrange("p (i o) -> p o i", o=PASSES),
            )

        for b in range(B):
            for j in range(GROUPS):
                first = b * N + j * P
                nc.tensor.transpose(turned[b][:, j, :], bias_row[:, first : first + P], identity[:])
            nc.scalar.copy(bias_cols[:, b * GROUPS : (b + 1) * GROUPS], turned[b][:, :, BIAS_ROW])
        for b in range(B):
            for j in range(GROUPS):
                col = b * GROUPS + j
                nc.tensor.transpose(
                    spread[b][:, j * P : (j + 1) * P], bias_cols[:, col : col + 1].to_broadcast([P, P]), identity[:]
                )
            nc.scalar.copy(bias[b][:], spread[b][:])

        nc.scalar.activation(grouped[0][:, :, 0], first_plane[:].indirect(query_list[:]), COPY)
        nc.scalar.activation(grouped[0][:, :, 1], plane_triple[:].indirect(query_list[:]), COPY)
        for t in range(2, PACK):
            nc.vector.tensor_copy(grouped[0][:, :, t], plane_triple[:, (t - 1) * POOL : t * POOL].indirect(query_list[:]))
        quantize(0, slice(0, QUERIES))
        nc.scalar.activation(grouped[1][:, :, 1], late_triple[:].indirect(query_list[:]), COPY)
        pieces = [slice(0, NQ // 2), slice(NQ // 2, NQ), slice(NQ, QUERIES)]
        for cols in pieces:
            entries = query_list[:, cols.start // 16 : cols.stop // 16]
            nc.scalar.activation(grouped[1][:, cols, 0], last_plane[:].indirect(entries), COPY)
        for b in range(B):
            q_cols = slice(b * NQ, (b + 1) * NQ)
            entries = query_list[:, b * NQ // 16 : (b + 1) * NQ // 16]
            for t in range(2, PACK):
                nc.vector.tensor_copy(picked[:, b, t - 2, :], late_triple[:, (t - 1) * POOL : t * POOL].indirect(entries))
        for b in range(B):
            nc.vector.tensor_copy(grouped[1][:, b * NQ : (b + 1) * NQ, 2:PACK], picked[:, b, :, :].rearrange("p t q -> p q t"))
        for cols in pieces:
            quantize(1, cols)

        for g in range(EARLY):
            multiply(0, g // GROUPS, g % GROUPS)
        for g in range(B * GROUPS):
            b, j = divmod(g, GROUPS)
            if g >= EARLY:
                multiply(0, b, j)
            multiply(1, b, j)
            add_bias(b, j)
            if g < 2:
                store(b, j, j + 1)
            elif j % 2 == 1:
                store(b, j - 1, j + 1)
